import numpy as np, ml_dtypes
CORES = [35,38,43,46]
N = 4
import mx_ref
BF = ml_dtypes.bfloat16
def gcols(t, e):
    v = np.concatenate([t.reshape(8, 16, -1, 4), np.zeros((8, 16, 1, 4), BF)], axis=2)
    return np.ascontiguousarray(np.stack([v[g][:, e[g]] for g in range(8)])).reshape(128, -1)
def tile(rs):
    return np.stack(rs, axis=2).reshape(128, -1).astype(BF)
def pick(q, e):
    c = np.concatenate([q[0].reshape(128, -1, 4), np.zeros((128, 1, 4), np.uint8)], axis=1); s = np.concatenate([q[1], np.ones((16, 1), np.uint8)], axis=1)
    return (np.ascontiguousarray(c[:, e].reshape(128, -1)), np.ascontiguousarray(s[:, e]))
def join(*qs):
    return (np.concatenate([q[0] for q in qs], axis=1), np.concatenate([q[1] for q in qs], axis=1))
def put(q, e, v):
    c, s = q[0].reshape(128, -1, 4).copy(), q[1].copy(); c[:, e] = v[0].reshape(128, -1, 4); s[:, e] = v[1]
    return (c.reshape(128, -1), s)
def pk(c, s):
    return (np.ascontiguousarray(c), mx_ref.live(s))
def emit(q):
    return q[0], q[1]
def packed(v, rng):
    q = [mx_ref.quantize(np.ascontiguousarray(v[r])) for r in range(N)]
    return np.stack([a for a, b in q]), np.stack([mx_ref.plane(b, rng) for a, b in q])
def values_of_codes():
    e, c = np.zeros((128, 128, 4), np.float32), np.zeros((128, 2, 4), np.uint8)
    e[np.arange(128), np.arange(128), 0] = 1
    c[:127, :, 0] = np.arange(256).reshape(2, 128).T[:127]
    return mx_ref.matmul(mx_ref.quantize(e.reshape(128, 512).astype(BF)), (c.reshape(128, 8), np.full((16, 2), 127, np.uint8))).T.reshape(-1).astype(np.float64)
CODE_VALUE, SCALE_VALUE = values_of_codes(), 2.0 ** (np.arange(256) - 127.0)
def decode(q):
    return (CODE_VALUE[q[0]].reshape(16, 8, -1, 4) * SCALE_VALUE[q[1]][:, None, :, None] + 0.0).reshape(128, -1).astype(np.float32)
def f(rng, *shape):
    return mx_ref.flush((rng.standard_normal(shape, dtype=np.float32) * np.exp2(rng.integers(-2, 3, shape[:-1] + (1,)))).astype(BF))
def wide(rng, *shape, cols=0):
    v = rng.standard_normal(shape, dtype=np.float32) * np.exp2(rng.integers(-12, 13, shape)).astype(np.float32)
    if cols: v *= np.repeat(np.exp2(rng.integers(-cols, cols + 1, shape[:-2] + (1, shape[-1] // 4))) * (rng.random(shape[:-2] + (1, shape[-1] // 4)) > 0.0625), 4, axis=-1).astype(np.float32)
    return mx_ref.flush(v.astype(BF))
C, R = 336, 2
def alike(w):
    return np.stack([w] * N)
def layers(rng):
    return f(rng, N, 128, 4096)
def weights(rng, w, still=()):
    w = np.array(w).reshape(N, 8, 16, 8, 8, 16, 4)
    for i in still:
        w[:, :, i] = 0
        w[:, :, :, :, :, i] = 0
    c, p = packed(w.reshape(N, 128, 4096), rng)
    return {"wc": c, "ws": p}
def numbers_of(rng):
    return {"x": np.array(f(rng, N, 128, 4 * C)), "u": alike(f(rng, 128, 512)), "v": np.array(f(rng, N, 128, 512))}
def unscored(rng):
    a = np.array(f(rng, 128, 512)).reshape(128, 128, 4)
    a[:, ::16] = 0
    a[:, 1::16] = 0
    return a
def setup_inputs(rng):
    return {**numbers_of(rng), **weights(rng, layers(rng))}
def setup_inputs_ties(rng):
    d = numbers_of(rng)
    o = rng.permutation(N)
    k = rng.integers(0, 3, (N, 8, C))
    m = np.where((o % 2 == 0)[:, None, None], k, rng.integers(-2, 3, (N, 8, C)))
    k[o == 0] = 0
    m[o == 0] = 0
    k[o == 1] *= -1
    x = d["x"].reshape(N, 8, 16, C, 4)
    x[:, :, 0] = 0
    x[:, :, 0, :, 0] = k.astype(np.float32).astype(BF)
    x[:, :, 0, :, 1] = m.astype(np.float32).astype(BF)
    a = unscored(rng)
    for h in range(0, 128, 16):
        a[h, h, 0] = 1
        a[h, h + 1, 1] = 1
    return {"x": x.reshape(N, 128, 4 * C), "u": alike(a.reshape(128, 512)), "v": d["v"], **weights(rng, layers(rng), [0])}
def setup_inputs_near(rng):
    d = numbers_of(rng)
    x = d["x"].astype(np.float32).reshape(N, 8, 16, C, 4)
    x[:, :, 0] = 0
    x[:, :, 8:] = 0
    a = unscored(rng)
    o = rng.permutation(8) % 4
    for g in range(8):
        h = 16 * g
        for m in range(2):
            s = rng.integers(0, 16, (N, C))
            c = rng.integers(0, 2, (N, C)) * 2.0 - 1.0
            if o[g] < 3: x[:, g, 8 + m] = ((s[:, :, None] >> np.arange(4)) & 1) * np.exp2(np.arange(4) - 23.0)
            if o[g] < 2:
                k = 1.0 if o[g] == 0 else 2.0 ** -30
                x[:, g, 0, :, m] = c
                x[:, g, 11, :, 0] = 2.0 ** -10
                a[h, h + m, m] = k
                a[h + 8 + m, h + m] = k
                a[h + 11, h + m, 0] = k
            elif o[g] == 2:
                for r in range(N): x[r, g, 0, rng.permutation(C)[:2], m] = [1.0, -1.0]
                a[h, h + m, m] = 2.0 ** 30
                a[h + 8 + m, h + m] = 2.0 ** -30
            else:
                x[:, g, 10, :, m] = np.where(s % 2 == 0, 1.125 * 2.0 ** -30 * c, 0.0)
                x[:, g, 12, :, m] = np.where(s % 2 == 0, 0.0, 1.25 * 2.0 ** -30 * c)
                a[h + 10, h + m, m] = 1.125 * 2.0 ** -30
                a[h + 12, h + m, m] = 2.0 ** -30
    return {"x": x.reshape(N, 128, 4 * C).astype(BF), "u": alike(a.reshape(128, 512)), "v": d["v"], **weights(rng, layers(rng), [0, 8, 9, 10, 11, 12, 13, 14, 15])}
def setup_inputs_odd(rng):
    d = numbers_of(rng)
    a = (1.0 + (2 * rng.integers(0, 64, (N, 16, 8, C, 4)) + 1) * 2.0 ** -7) * np.exp2(-rng.integers(8, 15, (N, 16, 8, C, 4)).astype(np.float64))
    a = np.where(np.arange(8)[:, None, None] * 4 + np.arange(4) == rng.integers(0, 32, (N, 16, 1, C, 1)), 1.96875, a)
    a = a * (rng.integers(0, 2, a.shape) * 2.0 - 1.0) * np.exp2(rng.integers(-2, 3, (N, 16, 1, C, 1)).astype(np.float64))
    return {"x": a.astype(np.float32).reshape(N, 128, 4 * C).astype(BF), "u": d["u"], "v": d["v"], **weights(rng, layers(rng), [8, 9, 10, 11, 12, 13, 14, 15])}
def setup_inputs_ends(rng):
    d = numbers_of(rng)
    o = rng.permutation(N) % 4
    x = np.zeros((N, 8, 16, C, 4), np.float32)
    x[:, :, 8:12] = f(rng, N, 8, 4, C, 4).astype(np.float32) * np.float32(1024)
    for r in range(N):
        c = rng.integers(0, 2, C) * 2.0 - 1.0
        w = rng.choice([1.375, 1.5], (8, C))
        a, b = rng.permutation(C)[:2]
        w[:, b] = 1.625
        if o[r] == 0:
            w[:, a] = 1.625
            c[a], c[b] = 1.0, -1.0
        else: w[:, a] = 1.25
        if o[r] == 1: c[:] = -1.0
        if o[r] == 2: c[:] = 1.0
        e = w * c * 2.0 ** 29 if o[r] < 2 else np.ones((8, 1)) * c * 2.0 ** -30
        x[r, :, :8] = e[:, None, :, None]
        k = (rng.integers(0, 2, (128, 512)) * 2.0 - 1.0).astype(np.float32)
        if o[r] == 1: d["v"][r] = (k * np.float32(2.0 ** 30)).astype(BF)
        if o[r] == 2: d["v"][r] = (k * np.float32(2.0 ** -30)).astype(BF)
    u = unscored(rng).reshape(8, 16, 128, 4)
    p = rng.permutation(8)
    for g in range(8):
        k = (2.0 ** 30 if p[g] < 4 else 2.0 ** -29) * (1.0 if p[g] % 2 == 0 else -1.0)
        for m in range(2):
            u[:, :8, 16 * g + m] = 0.75 * k * (1 - 2 * m)
            u[g, :8, 16 * g + m] = k * (1 - 2 * m)
    w = ((rng.integers(0, 2, (N, 128, 4096)) * 2.0 - 1.0) * 2.0 ** -11).astype(np.float32).astype(BF)
    return {"x": x.reshape(N, 128, 4 * C).astype(BF), "u": alike(u.reshape(128, 512)), "v": d["v"], **weights(rng, w, [0, 1, 2, 3, 4, 5, 6, 7])}
def setup_inputs_spread(rng):
    d = numbers_of(rng)
    w = np.array(mx_ref.flush((layers(rng).astype(np.float32) * np.float32(2.0 ** -7)).astype(BF)))
    x = np.array(wide(rng, N, 128, 4 * C, cols=3))
    e = int(rng.integers(N))
    x[e] = ((1.0 + 0.25 * rng.random((128, 4 * C))) * 2.0 ** 24).astype(np.float32).astype(BF)
    w[e ^ 1] = (-0.1875 - 0.0625 * rng.random((128, 4096))).astype(np.float32).astype(BF)
    return {"x": x, "u": d["u"], "v": d["v"], **weights(rng, w)}
def check_inputs(d):
    b = []
    for k in ("x", "u", "v"):
        a = np.abs(d[k].astype(np.float32))
        if not (np.isfinite(a).all() and ((a == 0) | (a >= 2.0 ** -30) & (a <= 2.0 ** 30)).all()): b.append("a value of " + k)
    if (d["u"] != d["u"][:1]).any(): b.append("u isn't the same on all ranks")
    none, least, most = [emit(mx_ref.quantize(np.full((128, 16), k, np.float32).astype(BF)))[1][0, 0] for k in (0.0, 2.0 ** -30, 2.0 ** 30)]
    size = 0.0
    for r in range(N):
        if ((d["wc"][r] == 0x7F) | (d["wc"][r] == 0xFF)).any(): b.append("wc: a code that is no number")
        s = mx_ref.live(d["ws"][r])
        if ((s != none) & ((s < least) | (s > most))).any(): b.append("ws: a scale out of range")
        if (((d["wc"][r].reshape(16, 8, -1, 4) & 0x7F) != 0) & (s == none)[:, None, :, None]).any(): b.append("wc: a code other than zero where the scale is that of zeros")
        size = max(size, float(np.abs(decode(pk(d["wc"][r], d["ws"][r]))).max()))
    if not float(np.abs(d["x"].astype(np.float32)).max()) * (1.0 + 20.0 * size) * (1.0 + 20.0 * size) <= 900000000.0: b.append("the sizes of x and W together")
    return b
def places(s):
    o = np.argsort(-s, axis=1, kind="stable")
    i = np.zeros(s.shape, np.int64)
    np.put_along_axis(i, o, np.broadcast_to(np.arange(C), s.shape), axis=1)
    return o, i
def reference(x, u, v, wc, ws):
    qu = [mx_ref.quantize(u[r]) for r in range(N)]
    lay = [pk(wc[r], ws[r]) for r in range(N)]
    now = [x[r] for r in range(N)]
    total = np.zeros((N, C), np.int64)
    for t in range(R):
        q = [mx_ref.quantize(now[r]) for r in range(N)]
        full = [decode(q[r]).astype(BF) for r in range(N)]
        s = [mx_ref.matmul(qu[r], q[r]) + np.float32(0.0) for r in range(N)]
        first = [places(s[r][::16]) for r in range(N)]
        second = [places(s[r][1::16])[1] for r in range(N)]
        made = [None] * N
        for r in range(N):
            e = r ^ (1 << t)
            total[r] = first[r][1][0]
            took = np.zeros((8, C), np.int64)
            for g in range(8):
                turn = places(total[r][None])[1][0]
                took[g] = first[e][0][g][turn]
                total[r] = total[r] + second[e][g][took[g]]
            z = mx_ref.quantize(gcols(full[e], took))
            p = [mx_ref.matmul(pick(lay[r], np.arange(128 * b, 128 * b + 128)), z) for b in range(8)]
            y = tile([np.maximum(p[b], p[b + 4]) * np.float32(0.03125) for b in range(4)])
            back = gcols(decode(mx_ref.quantize(y)).astype(BF), np.argsort(took, axis=1))
            made[e] = (full[e].astype(np.float32) + back.astype(np.float32)).astype(BF)
        now = made
    y, tot = np.zeros((N, 128, C), np.float32), np.zeros((N, 1, C), np.float32)
    oc, osc = np.zeros((N, 128, 4 * C), np.uint8), np.zeros((N, 16, C), np.uint8)
    for r in range(N):
        q = mx_ref.quantize(now[r])
        y[r] = mx_ref.matmul(mx_ref.quantize(v[r]), q)
        tot[r, 0] = total[r]
        oc[r], osc[r] = emit(q)
    return {"y": y, "tot": tot, "oc": oc, "osc": osc}

@@ -1,0 +1,510 @@
+from concourse.mybir import dt, AluOpType, ActivationFunctionType
+
+AL, AF = AluOpType, ActivationFunctionType
+C, R = 336, 2
+HV = [(0, 176), (176, 336)]
+LV = [(0, 11), (12, 22)]
+INF = float(2 ** 90)
+TINY = float(2.0 ** -120)
+BIG = float(2 ** 21)
+MAGIC = 1.5 * 2.0 ** 28
+OFF = 47
+
+SCRATCH = {}
+
+
+def _s(name, n, d="float32", where="sbuf"):
+    SCRATCH[name] = (where, [128, n], d)
+
+
+def _q(name, n):
+    _s(name + "q", n, "float8_e4m3fn_x4")
+    _s(name + "s", n, "uint8")
+
+
+CONST = ["EU0", "EU1", "EU2", "EU3", "EG", "EA", "ED"] + ["EP%d" % _k for _k in range(8)]
+for _n in ("xin", "xt0", "xt1", "Z", "Yp", "Ca", "Cb", "C5", "PT", "F", "G", "Y"):
+    _s(_n, 4 * C, "bfloat16")
+for _n in ("uin", "vin", "ones", "W2", "W3", "W4"):
+    _s(_n, 512, "bfloat16")
+_s("Eb", 512 * len(CONST), "bfloat16")
+_q("E", 128 * len(CONST))
+for _n in ("yt", "ym"):
+    _s(_n, 4 * 176)
+_s("P", 8 * C)
+_s("Lg", 8 * 22, "uint16")
+for _k in range(8):
+    _s("pb%d" % _k, 512, "float32", "psum")
+for _n, _k in (("u", 128), ("v", 128), ("uu", 256), ("wl", 1024), ("ca", C), ("cb", C), ("z", C), ("pp", C)):
+    _q(_n, _k)
+for _h in range(2):
+    _s("CD%d" % _h, 4 * (HV[_h][1] - HV[_h][0]), "bfloat16")
+    _q("cd%d" % _h, HV[_h][1] - HV[_h][0])
+    _s("sc%d" % _h, HV[_h][1] - HV[_h][0])
+    _s("V%d" % _h, C)
+    _s("df%d" % _h, C)
+for _t in range(R):
+    _q("rx%d" % _t, C)
+    _q("ry%d" % _t, C)
+    _q("y%d" % _t, C)
+    _s("ls%d" % _t, 44, "uint16")
+    _s("ll%d" % _t, 44, "uint16")
+    _s("NL%d" % _t, 22, "uint16")
+for _t in range(R + 1):
+    _q("x%d" % _t, C)
+for _n in ("jp", "ji", "d", "dn", "de", "k1", "k2", "k3", "JR", "MN", "MNd", "MH", "RH", "t1", "Hd", "sa", "oW", "iW",
+           "tm", "tb", "va", "SD", "ysb"):
+    _s(_n, C)
+_s("hi", C, "bfloat16")
+_s("lo", C, "bfloat16")
+_s("MD", 112)
+_s("x6", 22)
+_s("x7", 22)
+_s("pI", 4, "int32")
+_s("oI", 16, "int32")
+_s("oU", 16, "uint16")
+_s("ML", 22, "uint16")
+_s("bc", 32)
+
+SEMAPHORES = ["ve", "ac", "pe", "gp", "lx", "lu", "lv", "lw", "lz", "out", "loc"]
+SEMAPHORES += ["%s%d" % (a, t) for a in ("xa", "la", "nl", "ya", "yb") for t in range(R)]
+
+
+def rank_program(g, core, T, topo):
+    r = T.rank_of(core)
+    if r is None:
+        return
+    queue = {"ve": g.vector, "ac": g.scalar, "pe": g.tensor, "gp": g, "sy": g.sync}
+    tick = {"ve": 0, "ac": 0, "pe": 0, "gp": 0}
+    known = {e: {} for e in queue}
+    wr, rd, dcount, arr, sent = {}, {}, {}, {}, [0]
+
+    def deps(e, reads, writes, own=False):
+        want = {}
+        for k in reads:
+            for s, v in wr.get(k, {}).items():
+                want[s] = max(v, want.get(s, 0))
+        for k in list(writes) + [k for k in reads if k[:2] == "pb"]:
+            for tab in (wr, rd):
+                for s, v in tab.get(k, {}).items():
+                    if s != e or own or tab is rd and e != "pe" and k in writes:
+                        want[s] = max(v, want.get(s, 0))
+        for s, v in want.items():
+            if known[e].get(s, 0) < v:
+                queue[e].wait_ge(T.sem[s], v)
+                known[e][s] = v
+
+    def op(e, fn, reads, writes, own=False):
+        deps(e, reads, writes, own)
+        fn(queue[e]).then_inc(T.sem[e], 1)
+        tick[e] += 1
+        for k in reads:
+            rd.setdefault(k, {})[e] = tick[e]
+        for k in writes:
+            wr.setdefault(k, {})[e] = tick[e]
+
+    def dma(e, out, in_, sem, total, reads=(), writes=()):
+        deps(e, reads, writes)
+        queue[e].dma_start(out, in_).then_inc(T.sem[sem], 16)
+        dcount[sem] = dcount.get(sem, 0) + 16
+        for k in writes:
+            wr.setdefault(k, {})[sem] = total
+        for k in reads:
+            rd.setdefault(k, {})[sem] = total
+
+    def tt(out, a, b, o, reads, writes):
+        op("ve", lambda q: q.tensor_tensor(out, a, b, o), reads, writes)
+
+    def ts(out, a, s1, s2, o0, o1, reads, writes):
+        if o1 is None:
+            op("ve", lambda q: q.tensor_scalar(out, a, s1, None, o0), reads, writes)
+        else:
+            op("ve", lambda q: q.tensor_scalar(out, a, s1, s2, o0, o1), reads, writes)
+
+    def cp(out, a, reads, writes, own=False):
+        op("ve", lambda q: q.tensor_copy(out, a), reads, writes, own)
+
+    def fill(ap, c, key):
+        op("ve", lambda q: q.memset(ap, c), [], [key])
+
+    def scan(out, a, b, ini, o0, o1, reads, writes):
+        op("ve", lambda q: q.tensor_tensor_scan(out, a, b, ini, o0, o1), reads, writes)
+
+    def act(out, a, f, reads, writes, bias=None, scale=1.0):
+        if bias is None:
+            op("ac", lambda q: q.activation(out, a, f, scale=scale), reads, writes)
+        else:
+            op("ac", lambda q: q.activation(out, a, f, bias=bias, scale=scale), reads, writes)
+
+    def at(n):
+        return ("E", 128 * CONST.index(n)) if n in CONST else (n, 0)
+
+    def eb(n):
+        k = 512 * CONST.index(n)
+        return T.Eb[:, k:k + 512]
+
+    def pl(n, b, a=0, e=C):
+        return T[n][:, C * b + a:C * b + e]
+
+    def lg(k, h):
+        return T.Lg[:, 22 * k + LV[h][0]:22 * k + LV[h][1]]
+
+    def quant(name, a, b, src, reads):
+        n, o = at(name)
+        op("ve", lambda q: q.quantize_mx(T[n + "q"][:, o + a:o + b], T[n + "s"][:, o + a:o + b], src),
+           reads, [name + str(a)])
+
+    def mm(bank, n, st, sa, mv, ma, start, stop, reads):
+        w, o = at(st)
+        o += sa
+        op("pe", lambda q: q.matmul_mx(T[bank][:, 0:n], T[w + "q"][:, o:o + 128], T[w + "s"][:, o:o + 128],
+                                       T[mv + "q"][:, ma:ma + n], T[mv + "s"][:, ma:ma + n], start, stop),
+           reads, [bank])
+
+    def send(pc, out, in_, rsem, reads):
+        deps("gp", reads, ())
+        rid, pid, _e = topo.addr(pc)
+        g.remote_dma(out, in_, T.sem[rsem], T.sem.loc, pid, rid, topo.mask(core, pc))
+        sent[0] += len(topo.engines(core, pc))
+
+    def arrives(keys, sem, val):
+        for k in keys:
+            wr.setdefault(k, {})[sem] = val
+        arr[sem] = val
+
+    def part(t):
+        return T.cores[r ^ (1 << t)]
+
+    def ne(t):
+        return len(topo.engines(part(t), core))
+
+    def send_x(t):
+        send(part(t), T["rx%dq" % t][:].bitcast(dt.uint8), T["x%dq" % t][:].bitcast(dt.uint8), "xa%d" % t,
+             ["x%d0" % t, "x%d176" % t])
+        send(part(t), T["rx%ds" % t][:], T["x%ds" % t][:], "xa%d" % t, ["x%d0" % t])
+        arrives(["rx%d" % t], "xa%d" % t, 2 * ne(t))
+
+    dma("sy", T.xin[:], T.x[:], "lx", 16, (), ["xin"])
+    dma("ac", T.uin[:], T.u[:], "lu", 16, (), ["uin"])
+    dma("sy", T.wlq[:].bitcast(dt.uint8), T.wc[:], "lw", 16, (), ["w0"])
+    dma("sy", T.vin[:], T.v[:], "lv", 16, (), ["vin"])
+    dma("sy", T.wls[:], T.ws[:], "lz", 16, (), ["wsc"])
+    f32 = dict(allow_small_or_imprecise_dtypes=True)
+    bc = T.bc
+
+    def iota(ap, pat, base, cm, key, **k):
+        op("gp", lambda q: q.iota(ap, pat, base, cm, **k), [], [key])
+
+    def sel(ap, src, pat, o, fl, base, cm, reads, key):
+        op("gp", lambda q: q.affine_select(ap, src, pat, o, fl, base, cm), reads, [key])
+
+    iota(T.pI[:, 0:1], [[1, 1]], 0, 1, "pI")
+    iota(T.oI[:], [[1, 2], [16, 8]], 0, 0, "oI")
+    iota(T.jp[:], [[0, 21], [1, 16]], 0, 0, "jp", **f32)
+    fill(T.ones[:], 1.0, "ones")
+    fill(T.k3[:], INF, "k3")
+    for n, w in (("W4", (1.0, 1.0, 1.0, 0.5)), ("W3", (0.5, 0.5, 1.0, 0.0)), ("W2", (512.0, 512.0, 0.0, 0.0))):
+        for k in range(4):
+            ts(T[n][:, k::4], T.ones[:, 0:128], w[k], None, AL.mult, None, ["ones"], [n])
+    ts(T.pI[:, 1:2], T.pI[:, 0:1], 15, None, AL.bitwise_and, None, ["pI"], ["pI1"])
+    ts(T.pI[:, 2:3], T.pI[:, 0:1], 4, None, AL.arith_shift_right, None, ["pI"], ["pI2"])
+    cp(bc[:, 0:1], T.pI[:, 1:2], ["pI1"], ["i"])
+    cp(T.oU[:], T.oI[:], ["oI"], ["oU"])
+    ts(T.d[:], T.jp[:], bc[:, 0:1], None, AL.subtract, None, ["jp", "i"], ["d"])
+    act(T.de[:], T.d[:], AF.Abs, ["d"], ["de"])
+    act(T.de[:], T.de[:], AF.Relu, ["de"], ["de"], bias=1.0, scale=-1.0)
+    act(T.MH[:], T.de[:], AF.Identity, ["de"], ["MH"], bias=-INF, scale=2 * INF)
+    sel(T.RH[:], T.k3[:], [[0, 21], [1, 16]], AL.is_gt, -INF, 0, 0, ["k3"], "RH")
+    act(T.dn[:], T.d[:], AF.Sign, ["d"], ["dn"], scale=-1.0)
+    act(T.k1[:], T.dn[:], AF.Relu, ["dn"], ["k1"], scale=4096.0)
+    act(T.k2[:], T.de[:], AF.Copy, ["de"], ["k2"], scale=-1024.0)
+    cp(bc[:, 1:2], T.pI[:, 2:3], ["pI2"], ["g"])
+    ts(bc[:, 3:4], bc[:, 0:1], 0.0, -3072.0, AL.is_equal, AL.mult, ["i"], ["bn"])
+    ts(bc[:, 4:5], bc[:, 3:4], float(OFF), None, AL.add, None, ["bn"], ["bA"])
+    ts(bc[:, 5:6], bc[:, 3:4], -1.0, 335.0 - OFF, AL.mult, AL.add, ["bn"], ["b0"])
+    ts(bc[:, 6:7], bc[:, 3:4], -1.0, 1024.0, AL.mult, AL.add, ["bn"], ["ad"])
+    fill(bc[:, 24:25], -TINY, "tiny")
+    fill(bc[:, 25:26], TINY, "tiny")
+    quant("x0", 0, C, T.xin[:], ["xin"])
+    quant("u", 0, 128, T.uin[:], ["uin"])
+    cp(T.uuq[:].bitcast(dt.uint32), T.uq[:].bitcast(dt.uint32).indirect(T.oU[:]), ["u0", "oU"], ["uuc"])
+    cp(T.uus[:], T.us[:].indirect(T.oU[:]), ["u0", "oU"], ["uup"])
+    for pb in ("pb0", "pb7"):
+        mm(pb, C, "uu", 0, "x0", 0, True, True, ["uuc", "uup", "x00"])
+    sel(eb("EG"), T.W4[:], [[-16, 8], [0, 64]], AL.is_ge, 0.0, 0, 1, ["W4"], "EGb")
+    sel(eb("EG"), eb("EG"), [[16, 8], [0, 64]], AL.is_ge, 0.0, 15, -1, ["EGb"], "EGb")
+    sel(eb("EA"), T.W4[:], [[0, 512]], AL.is_ge, 0.0, 15, -1, ["W4"], "EAb")
+    send_x(0)
+    iota(T.ji[:], [[1, C]], 0, 0, "ji", **f32)
+    iota(T.JR[:], [[-1, C]], 512 * OFF + 511, 0, "JR", **f32)
+    for b in range(4):
+        sel(eb("EU%d" % b), T.ones[:], [[1, 512]], AL.is_equal, 0.0, -b, -4, ["ones"], "EU%db" % b)
+    sel(eb("ED"), T.W3[:], [[0, 512]], AL.is_ge, 0.0, 111, -1, ["W3"], "EDb")
+    fill(T.MD[:], BIG, "MD0")
+    sel(T.MD[:], T.MD[:], [[-1, 112]], AL.is_gt, 0.0, 0, 1, ["MD0"], "MD1")
+    sel(T.MD[:], T.MD[:], [[1, 112]], AL.not_equal, -BIG, 0, -1, ["MD1"], "MD")
+
+    def consts1():
+        quant("EG", 0, 128, eb("EG"), ["EGb"])
+        quant("EA", 0, 128, eb("EA"), ["EAb"])
+        for n, k, m in (("C5", 1, C), ("C5", 2, C), ("CD0", 3, 176), ("CD1", 3, 160), ("PT", 2, C), ("PT", 3, C)):
+            ts(T[n][:, k::4], T.ones[:, 0:m], 0.0, None, AL.mult, None, ["ones"], [n])
+
+    def consts2():
+        tt(T.MN[:], T.k1[:], T.k2[:], AL.add, ["k1", "k2"], ["MN"])
+        ts(T.MN[:, 15::16], T.MN[:, 15::16], bc[:, 6:7], None, AL.add, None, ["MN", "ad"], ["MN"])
+        for t in range(R):
+            fill(T["ls%d" % t][:], 0, "ls%d" % t)
+            fill(T["NL%d" % t][:], 0, "NL%d" % t)
+        for k in range(6):
+            fill(T.Lg[:, 22 * k + 11:22 * k + 12], 0, "Lp%d" % k)
+
+    def consts3():
+        for b in range(4):
+            quant("EU%d" % b, 0, 128, eb("EU%d" % b), ["EU%db" % b])
+        act(T.k3[:, 0:224], T.de[:, 0:224], AF.Copy, ["de", "RH"], ["k3"], scale=-1024.0 + 111.5)
+        act(T.k3[:, 224:C], T.de[:, 224:C], AF.Copy, ["de", "RH"], ["k3"], scale=-1024.0 + 112.0)
+        tt(T.MNd[:], T.k1[:], T.k3[:], AL.add, ["k1", "k3"], ["MNd"])
+        ts(T.MNd[:, 15::16], T.MNd[:, 15::16], bc[:, 6:7], None, AL.add, None, ["MNd", "ad"], ["MNd"])
+        ts(T.MD[:, 111:112], T.MD[:, 111:112], BIG, None, AL.add, None, ["MD"], ["MD"])
+        ts(bc[:, 9:10], bc[:, 1:2], 6.0, None, AL.is_equal, None, ["g"], ["m6"])
+        tt(bc[:, 10:11], bc[:, 9:10], bc[:, 3:4], AL.mult, ["m6", "bn"], ["mb"])
+        ts(bc[:, 11:12], bc[:, 9:10], 14096.0, -10000.0, AL.mult, AL.add, ["m6"], ["c6"])
+        tt(bc[:, 11:12], bc[:, 11:12], bc[:, 10:11], AL.add, ["c6", "mb"], ["c6"])
+        ts(bc[:, 12:13], bc[:, 9:10], -4096.0, bc[:, 3:4], AL.mult, AL.add, ["m6", "bn"], ["b7"])
+        tt(bc[:, 12:13], bc[:, 12:13], bc[:, 10:11], AL.subtract, ["b7", "mb"], ["b7"])
+        quant("ED", 0, 128, eb("ED"), ["EDb"])
+
+    def places(bank, counts, hook):
+        S = T[bank]
+        tt(T.t1[:], S[:, 0:C], T.MH[:], AL.min, [bank, "MH"], ["t1"])
+        scan(T.Hd[:], T.RH[:], T.t1[:], -INF, AL.min, AL.max, ["RH", "t1"], ["Hd"])
+        for q in range(6):
+            n = "C5" if q == 5 else ("Ca", "Cb")[q % 2]
+            for k in ((3, 0, 1, 2) if q < 5 else (3,)):
+                c = 4 * q + k if q < 5 else 20
+                m = 16 * (c + 1)
+                D = T.Hd[:, m - 1:m]
+                parts = [(0, m, AL.is_lt, 24), (m, C, AL.is_le, 25)][:1 if c == 20 else 2]
+                if k == 3:
+                    df = "df%d" % (q % 2)
+                    act(T[df][:], T.pb7[:, 0:C], AF.Identity, ["pb7", "Hd"], [df], bias=D, scale=-1.0)
+                    for a, e, o, z in parts:
+                        act(T[n][:, 4 * a + 3:4 * e:4], T[df][:, a:e], AF.Sign, [df, "tiny"], [n + ".s"],
+                            bias=bc[:, z:z + 1])
+                else:
+                    for a, e, o, z in parts:
+                        ts(T[n][:, 4 * a + k:4 * e:4], S[:, a:e], D, None, o, None, [bank, "Hd"], [n])
+            if q == 5:
+                tt(T[n][:, 0::4], S[:, 0:C], T.Hd[:], AL.is_equal, [bank, "Hd"], [n])
+            hook(q)
+            k = ("ca", "cb")[q % 2]
+            quant(k, 0, C, T[n][:], [n, n + ".s"])
+            for st, pb in counts:
+                mm(pb, C, st, 0, k, 0, q == 0, q == 5, [k + "0", st + "0"])
+
+    def to_list(src, key, bias, sign, outs, okey):
+        scan(T.sa[:], src, T.MN[:], 4096.0, AL.min, AL.add, [key, "MN"], ["sa"])
+        for o, a, b in outs:
+            ts(o, T.sa[:, 16 * a + 15:16 * b:16], sign, bias, AL.mult, AL.add, ["sa", "bn", "bA", "b0"], [okey])
+
+    for t in range(R):
+        pc, ls, ll, NL = part(t), T["ls%d" % t], T["ll%d" % t], T["NL%d" % t]
+        lk, X = "ls%d" % t, "x%d" % t
+        places("pb0", [("EG", "pb2"), ("EA", "pb3")], lambda q: consts1() if t == 0 and q == 0 else None)
+        if t == 0:
+            consts2()
+        for pb in ("pb1", "pb7"):
+            mm(pb, C, "uu", 128, "rx%d" % t, 0, True, True, ["uuc", "uup", "rx%d" % t])
+        to_list(T.pb2[:, 0:C], "pb2", bc[:, 4:5], 1.0, [(ls[:, 0:21], 0, 21)], lk)
+        cp(T.oW[:].indirect(ls[:, 0:21]), T.ji[:], [lk, "ji"], ["oW"])
+        to_list(T.oW[:], "oW", bc[:, 3:4], 1.0, [(ls[:, 22:43], 0, 21)], lk)
+        send(pc, ll[:], ls[:], "la%d" % t, [lk])
+        arrives(["ll%d" % t], "la%d" % t, ne(t))
+        if t == 0:
+            for k in range(8):
+                sel(eb("EP%d" % k), T.W2[:], [[0, 512]], AL.is_equal, 0.0, -16 * k, 1, ["W2"], "EP%db" % k)
+        act(T.va[:], T.pb3[:, 0:C], AF.Copy, ["pb3"], ["va"], scale=512.0)
+        to_list(T.pb3[:, 0:C], "pb3", bc[:, 5:6], -1.0, [(lg(0, 0), 0, 11), (lg(0, 1), 11, 21)], "Lg0")
+        tt(T.V0[:], T.va[:], T.JR[:], AL.add, ["va", "JR"], ["V0"])
+        if t == 0:
+            consts3()
+
+        def unpack(q):
+            if q < 4:
+                pb = ("pb4", "pb5", "pb6", "pb0")[q]
+                mm(pb, C, "EU%d" % q, 0, "rx%d" % t, 0, True, True, ["EU%d0" % q, "rx%d" % t])
+                act(pl("F", q), T[pb][:, 0:C], AF.Copy, [pb], ["F%d" % q])
+
+        places("pb1", [("EG", "pb2")], unpack)
+        if t == 0:
+            for k in range(8):
+                quant("EP%d" % k, 0, 128, eb("EP%d" % k), ["EP%db" % k])
+        ts(T.hi[:], T.pb2[:, 0:C], MAGIC, -MAGIC, AL.add, AL.add, ["pb2"], ["hi"])
+        tt(T.lo[:], T.pb2[:, 0:C], T.hi[:], AL.subtract, ["pb2", "hi"], ["lo"])
+        act(T.PT[:, 0::4], T.hi[:].indirect(ll[:, 22:43]), AF.Copy, ["hi", "PT", "ll%d" % t], ["PT0"])
+        cp(T.PT[:, 1::4], T.lo[:].indirect(ll[:, 22:43]), ["lo", "ll%d" % t], ["PT1"])
+        quant("pp", 0, C, T.PT[:], ["PT", "PT0", "PT1"])
+
+        def table(k):
+            pb = "pb%d" % (4 + k % 4)
+            mm(pb, C, "EP%d" % k, 0, "pp", 0, True, True, ["EP%d0" % k, "pp0"])
+            act(pl("P", k), T[pb][:, 0:C], AF.Copy, [pb], ["P%d" % k])
+
+        def sort(b):
+            act(pl("G", b), pl("F", b).indirect(ll[:, 22:43]), AF.Copy, ["F%d" % b, "ll%d" % t], ["G%d" % b])
+
+        def grow(k, h):
+            a, e = HV[h]
+            tt(T["V%d" % ((k + 1) % 2)][:, a:e], pl("P", k).indirect(lg(k, h)), T["V%d" % (k % 2)][:, a:e], AL.add,
+               ["P%d" % k, "Lg0" if k == 0 else "Lg%d.%d" % (k, h), "V%d" % (k % 2), "V%d.%d" % (k % 2, h)],
+               ["V%d.%d" % ((k + 1) % 2, h)])
+
+        def hold(k, s):
+            V = "V%d" % ((k + 1) % 2)
+            scan(T.SD[:, 112 * s:112 * s + 112], T[V][:, 112 * s:112 * s + 112], T.MD[:], BIG, AL.min, AL.add,
+                 ["MD", V + ".0"] + ([V + ".1"] if s else []), ["SD%d" % s])
+
+        table(0)
+        table(1)
+        grow(0, 0)
+        hold(0, 0)
+        grow(0, 1)
+        hold(0, 1)
+        hold(0, 2)
+        dma("sy", NL[0:16, :], T.Lg[0:16, 0:22], "nl%d" % t, 96, ["Lg0", "Lp0", "NL%d" % t], ["NLd%d" % t])
+        for k in range(1, 8):
+            V = "V%d" % (k % 2)
+            vk = [V + ".0", V + ".1"]
+            for h in range(2):
+                a, e = HV[h]
+                for s in range(2):
+                    act(T["CD%d" % h][:, s::4], T[V][:, a:e], AF.Sign, vk[0:1 + h] + ["SD%d" % s, "CD%d" % h],
+                        ["CD%d.%d" % (h, s)], bias=T.SD[:, 112 * s + 111:112 * s + 112], scale=-1.0)
+            if k < 7:
+                table(k + 1)
+            if 2 <= k < 6:
+                sort(k - 2)
+            for h in range(2):
+                a, e = HV[h]
+                ts(T["CD%d" % h][:, 2::4], T[V][:, a:e], T.SD[:, 335:336], None, AL.is_lt, None,
+                   vk + ["SD2"], ["CD%d.2" % h])
+                quant("cd%d" % h, 0, e - a, T["CD%d" % h][:], ["CD%d.%d" % (h, s) for s in range(3)])
+                mm("pb%d" % h, e - a, "ED", 0, "cd%d" % h, 0, True, True, ["ED0", "cd%d0" % h])
+            for h in range(2):
+                a, e = HV[h]
+                x, y = LV[h]
+                got = T["sc%d" % h]
+                scan(got[:], T["pb%d" % h][:, 0:e - a], T.MNd[:, a:e], 4096.0, AL.min, AL.add,
+                     ["pb%d" % h, "MNd"], ["sc%d" % h])
+                if k < 7 or t == R - 1:
+                    ts(lg(k, h), got[:, 15::16], bc[:, 3:4], None, AL.add, None, ["sc%d" % h, "bn"],
+                       ["Lg%d.%d" % (k, h)])
+                if k == 6:
+                    ts(T.x6[96:128, x:y], got[96:128, 15::16], bc[96:128, 9:10], bc[96:128, 11:12], AL.mult, AL.add,
+                       ["sc%d" % h, "m6", "c6"], ["x6.%d" % h])
+                if k == 7:
+                    tt(T.x7[96:128, x:y], got[96:128, 15::16], T.x6[96:128, x:y], AL.max,
+                       ["sc%d" % h, "x6.%d" % h], ["x7.%d" % h])
+                    ts(NL[96:128, x:y], T.x7[96:128, x:y], bc[96:128, 12:13], None, AL.add, None,
+                       ["x7.%d" % h, "b7", "NL%d" % t], ["NL%d.%d" % (t, h)])
+                if k < 7:
+                    grow(k, h)
+                    for s in ((0,), (1, 2))[h]:
+                        hold(k, s)
+            if k < 6:
+                dma("sy", NL[16 * k:16 * k + 16, :], T.Lg[16 * k:16 * k + 16, 22 * k:22 * k + 22], "nl%d" % t, 96,
+                    ["Lg%d.0" % k, "Lg%d.1" % k, "Lp%d" % k], [])
+        zk = [["NL%d" % t, "NL%d.%d" % (t, h), "NLd%d" % t] for h in range(2)]
+        for h in range(2):
+            a, e = HV[h]
+            x, y = LV[h]
+            for b in range(4):
+                o, i = T.Z[:, 4 * a + b:4 * e:4], pl("G", b).indirect(NL[:, x:y])
+                if b < 2:
+                    cp(o, i, ["G%d" % b] + zk[h], ["Z%d.%d" % (h, b)])
+                else:
+                    act(o, i, AF.Copy, ["G%d" % b] + zk[h], ["Z%d.%d" % (h, b)])
+            quant("z", a, e, T.Z[:, 4 * a:4 * e], ["Z%d.%d" % (h, b) for b in range(4)])
+
+        def layer(h):
+            a, e = HV[h]
+            for b in range(4):
+                for j in (1, 0):
+                    mm("pb%d" % (2 * b + j), e - a, "wl", 128 * (b + 4 * j), "z", a, True, True,
+                       ["w0", "wsc", "z%d" % a])
+                act(T.yt[:, 176 * b:176 * b + e - a], T["pb%d" % (2 * b + 1)][:, 0:e - a], AF.Copy,
+                    ["pb%d" % (2 * b + 1)], ["yt%d" % b])
+
+        def best(h):
+            a, e = HV[h]
+            for b in range(4):
+                m = T.ym[:, 176 * b:176 * b + e - a]
+                tt(m, T["pb%d" % (2 * b)][:, 0:e - a], T.yt[:, 176 * b:176 * b + e - a], AL.max,
+                   ["pb%d" % (2 * b), "yt%d" % b], ["ym%d" % b])
+                act(pl("Y", b, a, e), m, AF.Copy, ["ym%d" % b], ["Y%d.%d" % (b, h)], scale=0.03125)
+
+        layer(0)
+        for h in range(2):
+            cp(T.iW[:].indirect(NL[:, LV[h][0]:LV[h][1]]), T.ji[:, HV[h][0]:HV[h][1]], ["ji"] + zk[h], ["iW"], True)
+        best(0)
+        layer(1)
+        cp(T.tm[:], T.iW[:].indirect(ll[:, 0:21]), ["iW", "ll%d" % t], ["tm"])
+        to_list(T.tm[:], "tm", bc[:, 3:4], 1.0, [(T.ML[:, 0:11], 0, 11), (T.ML[:, 12:22], 11, 21)], "ML")
+        best(1)
+        for h in range(2):
+            a, e = HV[h]
+            x, y = LV[h]
+            for b in range(4):
+                o, i = T.Yp[:, 4 * a + b:4 * e:4], pl("Y", b).indirect(T.ML[:, x:y])
+                rk = ["ML", "Y%d.0" % b, "Y%d.1" % b]
+                if b < 3 - h:
+                    cp(o, i, rk, ["Yp%d.%d" % (h, b)])
+                else:
+                    act(o, i, AF.Copy, rk, ["Yp%d.%d" % (h, b)])
+            quant("y%d" % t, a, e, T.Yp[:, 4 * a:4 * e], ["Yp%d.%d" % (h, b) for b in range(4)])
+            k, sm = ["y%d%d" % (t, a)], ("ya%d", "yb%d")[h] % t
+            send(pc, T["ry%dq" % t][:, a:e].bitcast(dt.uint8), T["y%dq" % t][:, a:e].bitcast(dt.uint8), sm, k)
+            send(pc, T["ry%ds" % t][:, a:e], T["y%ds" % t][:, a:e], sm, k)
+            arrives(["ry%d.%d" % (t, h)], sm, 2 * ne(t))
+        for h in range(2):
+            a, e = HV[h]
+            for b in range(4):
+                mm("pb%d" % (4 * h + b), e - a, "EU%d" % b, 0, X, a, True, False, ["EU%d0" % b, X + "0", X + "176"])
+        if t == R - 1:
+            grow(7, 0)
+            grow(7, 1)
+            tt(T.tb[0:1, :], T.V0[0:1, :], T.JR[0:1, :], AL.subtract, ["V0.0", "V0.1", "JR"], ["tb"])
+            ts(T.tb[0:1, :], T.tb[0:1, :], 2.0 ** -9, 9.0 * OFF, AL.mult, AL.add, ["tb"], ["tb"])
+            dma("sy", T.tot[:], T.tb[0:1, :], "out", 0, ["tb"], [])
+            quant("v", 0, 128, T.vin[:], ["vin"])
+        N, xt = "x%d" % (t + 1), T["xt%d" % t]
+        for h in range(2):
+            a, e = HV[h]
+            for b in range(4):
+                pb = "pb%d" % (4 * h + b)
+                mm(pb, e - a, "EU%d" % b, 0, "ry%d" % t, a, False, True, ["ry%d.%d" % (t, h)])
+                o = xt[:, 4 * a + b:4 * e:4]
+                if b > 0:
+                    cp(o, T[pb][:, 0:e - a], [pb], ["xt%d.%d" % (h, b)])
+                else:
+                    act(o, T[pb][:, 0:e - a], AF.Copy, [pb], ["xt%d.%d" % (h, b)])
+            quant(N, a, e, xt[:, 4 * a:4 * e], ["xt%d.%d" % (h, b) for b in range(4)])
+        if t < R - 1:
+            send_x(t + 1)
+            for pb in ("pb0", "pb7"):
+                mm(pb, C, "uu", 0, N, 0, True, True, [N + "0", N + "176"])
+    nk = ["x20", "x2176"]
+    mm("pb0", C, "v", 0, "x2", 0, True, True, ["v0"] + nk)
+    dma("sy", T.oc[:], T.x2q[:].bitcast(dt.uint8), "out", 0, nk, [])
+    act(T.ysb[:], T.pb0[:, 0:C], AF.Copy, ["pb0"], ["ysb"])
+    for k in range(4):
+        dma("sy", T.osc[4 * k:4 * k + 4, :], T.x2s[32 * k:32 * k + 4, :], "out", 0, nk, [])
+    dma("ac", T.y[:], T.ysb[:], "out", 0, ["ysb"], [])
+    for s in tick:
+        g.wait_ge(T.sem[s], tick[s])
+    for s in dcount:
+        g.wait_ge(T.sem[s], dcount[s])
+    for s in arr:
+        g.wait_ge(T.sem[s], arr[s])
+    g.wait_ge(T.sem.loc, sent[0])

@@ -2,8 +2,8 @@ from concourse.mybir import dt, AluOpType, ActivationFunctionType
 
 AL, AF = AluOpType, ActivationFunctionType
 C, R = 336, 2
-HV = [(0, 176), (176, 336)]
-LV = [(0, 11), (12, 22)]
+HV = [(0, 160), (160, 336)]
+LV = [(0, 10), (10, 21)]
 INF = float(2 ** 90)
 TINY = float(2.0 ** -120)
 BIG = float(2 ** 21)
@@ -40,7 +40,6 @@ for _n, _k in (("u", 128), ("v", 128), ("uu", 256), ("wl", 1024), ("ca", C), ("c
 for _h in range(2):
     _s("CD%d" % _h, 4 * (HV[_h][1] - HV[_h][0]), "bfloat16")
     _q("cd%d" % _h, HV[_h][1] - HV[_h][0])
-    _s("sc%d" % _h, HV[_h][1] - HV[_h][0])
     _s("V%d" % _h, C)
     _s("df%d" % _h, C)
 for _t in range(R):
@@ -53,7 +52,7 @@ for _t in range(R):
 for _t in range(R + 1):
     _q("x%d" % _t, C)
 for _n in ("jp", "ji", "d", "dn", "de", "k1", "k2", "k3", "JR", "MN", "MNd", "MH", "RH", "t1", "Hd", "sa", "oW", "iW",
-           "tm", "tb", "va", "SD", "ysb"):
+           "tm", "tb", "va", "SD", "ysb", "sc"):
     _s(_n, C)
 _s("hi", C, "bfloat16")
 _s("lo", C, "bfloat16")
@@ -79,7 +78,7 @@ def rank_program(g, core, T, topo):
     known = {e: {} for e in queue}
     wr, rd, dcount, arr, sent = {}, {}, {}, {}, [0]
 
-    def deps(e, reads, writes, own=False):
+    def deps(e, reads, writes):
         want = {}
         for k in reads:
             for s, v in wr.get(k, {}).items():
@@ -87,15 +86,15 @@ def rank_program(g, core, T, topo):
         for k in list(writes) + [k for k in reads if k[:2] == "pb"]:
             for tab in (wr, rd):
                 for s, v in tab.get(k, {}).items():
-                    if s != e or own or tab is rd and e != "pe" and k in writes:
+                    if s != e or tab is rd and e != "pe" and k in writes:
                         want[s] = max(v, want.get(s, 0))
         for s, v in want.items():
             if known[e].get(s, 0) < v:
                 queue[e].wait_ge(T.sem[s], v)
                 known[e][s] = v
 
-    def op(e, fn, reads, writes, own=False):
-        deps(e, reads, writes, own)
+    def op(e, fn, reads, writes):
+        deps(e, reads, writes)
         fn(queue[e]).then_inc(T.sem[e], 1)
         tick[e] += 1
         for k in reads:
@@ -121,8 +120,8 @@ def rank_program(g, core, T, topo):
         else:
             op("ve", lambda q: q.tensor_scalar(out, a, s1, s2, o0, o1), reads, writes)
 
-    def cp(out, a, reads, writes, own=False):
-        op("ve", lambda q: q.tensor_copy(out, a), reads, writes, own)
+    def cp(out, a, reads, writes):
+        op("ve", lambda q: q.tensor_copy(out, a), reads, writes)
 
     def fill(ap, c, key):
         op("ve", lambda q: q.memset(ap, c), [], [key])
@@ -130,24 +129,18 @@ def rank_program(g, core, T, topo):
     def scan(out, a, b, ini, o0, o1, reads, writes):
         op("ve", lambda q: q.tensor_tensor_scan(out, a, b, ini, o0, o1), reads, writes)
 
-    def act(out, a, f, reads, writes, bias=None, scale=1.0):
-        if bias is None:
-            op("ac", lambda q: q.activation(out, a, f, scale=scale), reads, writes)
-        else:
-            op("ac", lambda q: q.activation(out, a, f, bias=bias, scale=scale), reads, writes)
+    def act(out, a, f, reads, writes, **k):
+        op("ac", lambda q: q.activation(out, a, f, **k), reads, writes)
 
     def at(n):
         return ("E", 128 * CONST.index(n)) if n in CONST else (n, 0)
 
-    def eb(n):
+    def eb(n, m=1):
         k = 512 * CONST.index(n)
-        return T.Eb[:, k:k + 512]
+        return T.Eb[:, k:k + 512 * m]
 
     def pl(n, b, a=0, e=C):
         return T[n][:, C * b + a:C * b + e]
-
-    def lg(k, h):
-        return T.Lg[:, 22 * k + LV[h][0]:22 * k + LV[h][1]]
 
     def quant(name, a, b, src, reads):
         n, o = at(name)
@@ -180,7 +173,7 @@ def rank_program(g, core, T, topo):
 
     def send_x(t):
         send(part(t), T["rx%dq" % t][:].bitcast(dt.uint8), T["x%dq" % t][:].bitcast(dt.uint8), "xa%d" % t,
-             ["x%d0" % t, "x%d176" % t])
+             ["x%d0" % t, "x%d160" % t])
         send(part(t), T["rx%ds" % t][:], T["x%ds" % t][:], "xa%d" % t, ["x%d0" % t])
         arrives(["rx%d" % t], "xa%d" % t, 2 * ne(t))
 
@@ -203,9 +196,8 @@ def rank_program(g, core, T, topo):
     iota(T.jp[:], [[0, 21], [1, 16]], 0, 0, "jp", **f32)
     fill(T.ones[:], 1.0, "ones")
     fill(T.k3[:], INF, "k3")
-    for n, w in (("W4", (1.0, 1.0, 1.0, 0.5)), ("W3", (0.5, 0.5, 1.0, 0.0)), ("W2", (512.0, 512.0, 0.0, 0.0))):
-        for k in range(4):
-            ts(T[n][:, k::4], T.ones[:, 0:128], w[k], None, AL.mult, None, ["ones"], [n])
+    fill(T.W4[:], 1.0, "W4")
+    ts(T.W4[:, 3::4], T.W4[:, 3::4], 0.5, None, AL.mult, None, ["W4"], ["W4"])
     ts(T.pI[:, 1:2], T.pI[:, 0:1], 15, None, AL.bitwise_and, None, ["pI"], ["pI1"])
     ts(T.pI[:, 2:3], T.pI[:, 0:1], 4, None, AL.arith_shift_right, None, ["pI"], ["pI2"])
     cp(bc[:, 0:1], T.pI[:, 1:2], ["pI1"], ["i"])
@@ -220,15 +212,14 @@ def rank_program(g, core, T, topo):
     act(T.k2[:], T.de[:], AF.Copy, ["de"], ["k2"], scale=-1024.0)
     cp(bc[:, 1:2], T.pI[:, 2:3], ["pI2"], ["g"])
     ts(bc[:, 3:4], bc[:, 0:1], 0.0, -3072.0, AL.is_equal, AL.mult, ["i"], ["bn"])
-    ts(bc[:, 4:5], bc[:, 3:4], float(OFF), None, AL.add, None, ["bn"], ["bA"])
-    ts(bc[:, 5:6], bc[:, 3:4], -1.0, 335.0 - OFF, AL.mult, AL.add, ["bn"], ["b0"])
-    ts(bc[:, 6:7], bc[:, 3:4], -1.0, 1024.0, AL.mult, AL.add, ["bn"], ["ad"])
+    for k, sg, b in ((4, 1.0, float(OFF)), (5, -1.0, 335.0 - OFF), (6, -1.0, 1024.0)):
+        act(bc[:, k:k + 1], bc[:, 3:4], AF.Identity, ["bn"], ["b%d" % k], bias=b, scale=sg)
     fill(bc[:, 24:25], -TINY, "tiny")
     fill(bc[:, 25:26], TINY, "tiny")
-    quant("x0", 0, C, T.xin[:], ["xin"])
     quant("u", 0, 128, T.uin[:], ["uin"])
     cp(T.uuq[:].bitcast(dt.uint32), T.uq[:].bitcast(dt.uint32).indirect(T.oU[:]), ["u0", "oU"], ["uuc"])
-    cp(T.uus[:], T.us[:].indirect(T.oU[:]), ["u0", "oU"], ["uup"])
+    act(T.uus[:], T.us[:].indirect(T.oU[:]), AF.Copy, ["u0", "oU"], ["uup"])
+    quant("x0", 0, C, T.xin[:], ["xin"])
     for pb in ("pb0", "pb7"):
         mm(pb, C, "uu", 0, "x0", 0, True, True, ["uuc", "uup", "x00"])
     sel(eb("EG"), T.W4[:], [[-16, 8], [0, 64]], AL.is_ge, 0.0, 0, 1, ["W4"], "EGb")
@@ -239,46 +230,59 @@ def rank_program(g, core, T, topo):
     iota(T.JR[:], [[-1, C]], 512 * OFF + 511, 0, "JR", **f32)
     for b in range(4):
         sel(eb("EU%d" % b), T.ones[:], [[1, 512]], AL.is_equal, 0.0, -b, -4, ["ones"], "EU%db" % b)
-    sel(eb("ED"), T.W3[:], [[0, 512]], AL.is_ge, 0.0, 111, -1, ["W3"], "EDb")
     fill(T.MD[:], BIG, "MD0")
     sel(T.MD[:], T.MD[:], [[-1, 112]], AL.is_gt, 0.0, 0, 1, ["MD0"], "MD1")
     sel(T.MD[:], T.MD[:], [[1, 112]], AL.not_equal, -BIG, 0, -1, ["MD1"], "MD")
 
-    def consts1():
-        quant("EG", 0, 128, eb("EG"), ["EGb"])
-        quant("EA", 0, 128, eb("EA"), ["EAb"])
-        for n, k, m in (("C5", 1, C), ("C5", 2, C), ("CD0", 3, 176), ("CD1", 3, 160), ("PT", 2, C), ("PT", 3, C)):
-            ts(T[n][:, k::4], T.ones[:, 0:m], 0.0, None, AL.mult, None, ["ones"], [n])
+    def consts1(q):
+        if q == 0:
+            quant("EG", 0, 256, eb("EG", 2), ["EGb", "EAb"])
+        zeros = [("C5", 1, C), ("C5", 2, C)] if q == 1 else []
+        if q == 4:
+            zeros = [("CD0", 3, 160), ("CD1", 3, 176), ("PT", 2, C), ("PT", 3, C)]
+        for n, k, m in zeros:
+            act(T[n][:, k::4], T.ones[:, 0:m], AF.Copy, ["ones"], [n + "z"], scale=0.0)
+        if q in (2, 3):
+            n, w = (("W3", (0.5, 0.5, 1.0, 0.0)), ("W2", (512.0, 512.0, 0.0, 0.0)))[q - 2]
+            for k in range(4):
+                act(T[n][:, k::4], T.ones[:, 0:128], AF.Copy, ["ones"], [n], scale=w[k])
 
     def consts2():
         tt(T.MN[:], T.k1[:], T.k2[:], AL.add, ["k1", "k2"], ["MN"])
-        ts(T.MN[:, 15::16], T.MN[:, 15::16], bc[:, 6:7], None, AL.add, None, ["MN", "ad"], ["MN"])
+        ts(T.MN[:, 15::16], T.MN[:, 15::16], bc[:, 6:7], None, AL.add, None, ["MN", "b6"], ["MN"])
         for t in range(R):
             fill(T["ls%d" % t][:], 0, "ls%d" % t)
-            fill(T["NL%d" % t][:], 0, "NL%d" % t)
-        for k in range(6):
-            fill(T.Lg[:, 22 * k + 11:22 * k + 12], 0, "Lp%d" % k)
 
     def consts3():
-        for b in range(4):
-            quant("EU%d" % b, 0, 128, eb("EU%d" % b), ["EU%db" % b])
-        act(T.k3[:, 0:224], T.de[:, 0:224], AF.Copy, ["de", "RH"], ["k3"], scale=-1024.0 + 111.5)
-        act(T.k3[:, 224:C], T.de[:, 224:C], AF.Copy, ["de", "RH"], ["k3"], scale=-1024.0 + 112.0)
+        quant("EU0", 0, 512, eb("EU0", 4), ["EU%db" % b for b in range(4)])
+        act(T.k3[:, 0:160], T.de[:, 0:160], AF.Copy, ["de", "RH"], ["k3"], scale=-1024.0 + 111.5)
+        act(T.k3[:, 160:C], T.de[:, 160:C], AF.Copy, ["de", "RH"], ["k3"], scale=-1024.0 + 56.0)
         tt(T.MNd[:], T.k1[:], T.k3[:], AL.add, ["k1", "k3"], ["MNd"])
-        ts(T.MNd[:, 15::16], T.MNd[:, 15::16], bc[:, 6:7], None, AL.add, None, ["MNd", "ad"], ["MNd"])
+        ts(T.MNd[:, 15::16], T.MNd[:, 15::16], bc[:, 6:7], None, AL.add, None, ["MNd", "b6"], ["MNd"])
         ts(T.MD[:, 111:112], T.MD[:, 111:112], BIG, None, AL.add, None, ["MD"], ["MD"])
-        ts(bc[:, 9:10], bc[:, 1:2], 6.0, None, AL.is_equal, None, ["g"], ["m6"])
-        tt(bc[:, 10:11], bc[:, 9:10], bc[:, 3:4], AL.mult, ["m6", "bn"], ["mb"])
-        ts(bc[:, 11:12], bc[:, 9:10], 14096.0, -10000.0, AL.mult, AL.add, ["m6"], ["c6"])
-        tt(bc[:, 11:12], bc[:, 11:12], bc[:, 10:11], AL.add, ["c6", "mb"], ["c6"])
-        ts(bc[:, 12:13], bc[:, 9:10], -4096.0, bc[:, 3:4], AL.mult, AL.add, ["m6", "bn"], ["b7"])
-        tt(bc[:, 12:13], bc[:, 12:13], bc[:, 10:11], AL.subtract, ["b7", "mb"], ["b7"])
+        act(bc[:, 8:9], bc[:, 1:2], AF.Identity, ["g"], ["g6"], bias=-6.0)
+        act(bc[:, 8:9], bc[:, 8:9], AF.Abs, ["g6"], ["g6"])
+        act(bc[:, 9:10], bc[:, 8:9], AF.Relu, ["g6"], ["m6"], bias=1.0, scale=-1.0)
+        act(bc[:, 10:11], bc[:, 9:10], AF.Copy, ["m6", "bn"], ["mb"], scale=bc[:, 3:4])
+        act(bc[:, 11:12], bc[:, 9:10], AF.Identity, ["m6", "mb"], ["c6"], bias=bc[:, 10:11], scale=14096.0)
+        act(bc[:, 11:12], bc[:, 11:12], AF.Identity, ["c6"], ["c6"], bias=-10000.0)
+        act(bc[:, 12:13], bc[:, 9:10], AF.Identity, ["m6", "bn"], ["b7"], bias=bc[:, 3:4], scale=-4096.0)
+        act(bc[:, 13:14], bc[:, 10:11], AF.Copy, ["mb"], ["nb"], scale=-1.0)
+        act(bc[:, 12:13], bc[:, 12:13], AF.Identity, ["b7", "nb"], ["b7"], bias=bc[:, 13:14])
         quant("ED", 0, 128, eb("ED"), ["EDb"])
 
     def places(bank, counts, hook):
         S = T[bank]
         tt(T.t1[:], S[:, 0:C], T.MH[:], AL.min, [bank, "MH"], ["t1"])
         scan(T.Hd[:], T.RH[:], T.t1[:], -INF, AL.min, AL.max, ["RH", "t1"], ["Hd"])
+
+        def count(q):
+            n, k = ("C5" if q == 5 else ("Ca", "Cb")[q % 2]), ("ca", "cb")[q % 2]
+            hook(q)
+            quant(k, 0, C, T[n][:], [n + ".0", n + ".1", n + ".2", n + ".3"] + (["C5z"] if q == 5 else []))
+            for st, pb in counts:
+                mm(pb, C, st, 0, k, 0, q == 0, q == 5, [k + "0", "EG0"])
+
         for q in range(6):
             n = "C5" if q == 5 else ("Ca", "Cb")[q % 2]
             for k in ((3, 0, 1, 2) if q < 5 else (3,)):
@@ -290,141 +294,145 @@ def rank_program(g, core, T, topo):
                     df = "df%d" % (q % 2)
                     act(T[df][:], T.pb7[:, 0:C], AF.Identity, ["pb7", "Hd"], [df], bias=D, scale=-1.0)
                     for a, e, o, z in parts:
-                        act(T[n][:, 4 * a + 3:4 * e:4], T[df][:, a:e], AF.Sign, [df, "tiny"], [n + ".s"],
+                        act(T[n][:, 4 * a + 3:4 * e:4], T[df][:, a:e], AF.Sign, [df, "tiny"], [n + ".3"],
                             bias=bc[:, z:z + 1])
                 else:
                     for a, e, o, z in parts:
-                        ts(T[n][:, 4 * a + k:4 * e:4], S[:, a:e], D, None, o, None, [bank, "Hd"], [n])
+                        ts(T[n][:, 4 * a + k:4 * e:4], S[:, a:e], D, None, o, None, [bank, "Hd"], [n + ".%d" % k])
+                    if k == 0 and q:
+                        count(q - 1)
             if q == 5:
-                tt(T[n][:, 0::4], S[:, 0:C], T.Hd[:], AL.is_equal, [bank, "Hd"], [n])
-            hook(q)
-            k = ("ca", "cb")[q % 2]
-            quant(k, 0, C, T[n][:], [n, n + ".s"])
-            for st, pb in counts:
-                mm(pb, C, st, 0, k, 0, q == 0, q == 5, [k + "0", st + "0"])
+                tt(T[n][:, 0::4], S[:, 0:C], T.Hd[:], AL.is_equal, [bank, "Hd"], [n + ".0"])
+                count(4)
+                count(5)
 
-    def to_list(src, key, bias, sign, outs, okey):
+    def to_list(src, key, bias, sign, o, okey):
         scan(T.sa[:], src, T.MN[:], 4096.0, AL.min, AL.add, [key, "MN"], ["sa"])
-        for o, a, b in outs:
-            ts(o, T.sa[:, 16 * a + 15:16 * b:16], sign, bias, AL.mult, AL.add, ["sa", "bn", "bA", "b0"], [okey])
+        ts(o, T.sa[:, 15::16], sign, bias, AL.mult, AL.add, ["sa", "bn", "b4", "b5"], [okey])
 
     for t in range(R):
         pc, ls, ll, NL = part(t), T["ls%d" % t], T["ll%d" % t], T["NL%d" % t]
         lk, X = "ls%d" % t, "x%d" % t
-        places("pb0", [("EG", "pb2"), ("EA", "pb3")], lambda q: consts1() if t == 0 and q == 0 else None)
+        places("pb0", [("EG", "pb2"), ("EA", "pb3")], lambda q: consts1(q) if t == 0 else None)
         if t == 0:
             consts2()
         for pb in ("pb1", "pb7"):
             mm(pb, C, "uu", 128, "rx%d" % t, 0, True, True, ["uuc", "uup", "rx%d" % t])
-        to_list(T.pb2[:, 0:C], "pb2", bc[:, 4:5], 1.0, [(ls[:, 0:21], 0, 21)], lk)
+        to_list(T.pb2[:, 0:C], "pb2", bc[:, 4:5], 1.0, ls[:, 0:21], lk)
         cp(T.oW[:].indirect(ls[:, 0:21]), T.ji[:], [lk, "ji"], ["oW"])
-        to_list(T.oW[:], "oW", bc[:, 3:4], 1.0, [(ls[:, 22:43], 0, 21)], lk)
+        to_list(T.oW[:], "oW", bc[:, 3:4], 1.0, ls[:, 22:43], lk)
         send(pc, ll[:], ls[:], "la%d" % t, [lk])
         arrives(["ll%d" % t], "la%d" % t, ne(t))
         if t == 0:
+            sel(eb("ED"), T.W3[:], [[0, 512]], AL.is_ge, 0.0, 111, -1, ["W3"], "EDb")
             for k in range(8):
                 sel(eb("EP%d" % k), T.W2[:], [[0, 512]], AL.is_equal, 0.0, -16 * k, 1, ["W2"], "EP%db" % k)
         act(T.va[:], T.pb3[:, 0:C], AF.Copy, ["pb3"], ["va"], scale=512.0)
-        to_list(T.pb3[:, 0:C], "pb3", bc[:, 5:6], -1.0, [(lg(0, 0), 0, 11), (lg(0, 1), 11, 21)], "Lg0")
-        tt(T.V0[:], T.va[:], T.JR[:], AL.add, ["va", "JR"], ["V0"])
+        to_list(T.pb3[:, 0:C], "pb3", bc[:, 5:6], -1.0, T.Lg[:, 0:21], "Lg0")
+        tt(T.V0[:], T.va[:], T.JR[:], AL.add, ["va", "JR"], ["V0.0", "V0.1"])
         if t == 0:
             consts3()
 
         def unpack(q):
             if q < 4:
                 pb = ("pb4", "pb5", "pb6", "pb0")[q]
-                mm(pb, C, "EU%d" % q, 0, "rx%d" % t, 0, True, True, ["EU%d0" % q, "rx%d" % t])
+                mm(pb, C, "EU%d" % q, 0, "rx%d" % t, 0, True, True, ["EU00", "rx%d" % t])
                 act(pl("F", q), T[pb][:, 0:C], AF.Copy, [pb], ["F%d" % q])
 
         places("pb1", [("EG", "pb2")], unpack)
         if t == 0:
-            for k in range(8):
-                quant("EP%d" % k, 0, 128, eb("EP%d" % k), ["EP%db" % k])
+            for k in (0, 4):
+                quant("EP%d" % k, 0, 512, eb("EP%d" % k, 4), ["EP%db" % (k + i) for i in range(4)])
         ts(T.hi[:], T.pb2[:, 0:C], MAGIC, -MAGIC, AL.add, AL.add, ["pb2"], ["hi"])
         tt(T.lo[:], T.pb2[:, 0:C], T.hi[:], AL.subtract, ["pb2", "hi"], ["lo"])
-        act(T.PT[:, 0::4], T.hi[:].indirect(ll[:, 22:43]), AF.Copy, ["hi", "PT", "ll%d" % t], ["PT0"])
+        act(T.PT[:, 0::4], T.hi[:].indirect(ll[:, 22:43]), AF.Copy, ["hi", "ll%d" % t], ["PT0"])
         cp(T.PT[:, 1::4], T.lo[:].indirect(ll[:, 22:43]), ["lo", "ll%d" % t], ["PT1"])
-        quant("pp", 0, C, T.PT[:], ["PT", "PT0", "PT1"])
+        quant("pp", 0, C, T.PT[:], ["PTz", "PT0", "PT1"])
 
         def table(k):
             pb = "pb%d" % (4 + k % 4)
-            mm(pb, C, "EP%d" % k, 0, "pp", 0, True, True, ["EP%d0" % k, "pp0"])
+            mm(pb, C, "EP%d" % k, 0, "pp", 0, True, True, ["EP%d0" % (k // 4 * 4), "pp0"])
             act(pl("P", k), T[pb][:, 0:C], AF.Copy, [pb], ["P%d" % k])
 
         def sort(b):
             act(pl("G", b), pl("F", b).indirect(ll[:, 22:43]), AF.Copy, ["F%d" % b, "ll%d" % t], ["G%d" % b])
 
-        def grow(k, h):
-            a, e = HV[h]
-            tt(T["V%d" % ((k + 1) % 2)][:, a:e], pl("P", k).indirect(lg(k, h)), T["V%d" % (k % 2)][:, a:e], AL.add,
-               ["P%d" % k, "Lg0" if k == 0 else "Lg%d.%d" % (k, h), "V%d" % (k % 2), "V%d.%d" % (k % 2, h)],
-               ["V%d.%d" % ((k + 1) % 2, h)])
+        def grow(k):
+            old, new = "V%d" % (k % 2), "V%d" % ((k + 1) % 2)
+            for h in range(2):
+                a, e = HV[h]
+                tt(T[new][:, a:e], pl("P", k).indirect(T.Lg[:, 22 * k + LV[h][0]:22 * k + LV[h][1]]), T[old][:, a:e],
+                   AL.add, ["P%d" % k, "Lg%d.%d" % (k, h) if k else "Lg0", old + ".%d" % h], [new + ".%d" % h])
 
-        def hold(k, s):
+        def hold(k):
             V = "V%d" % ((k + 1) % 2)
-            scan(T.SD[:, 112 * s:112 * s + 112], T[V][:, 112 * s:112 * s + 112], T.MD[:], BIG, AL.min, AL.add,
-                 ["MD", V + ".0"] + ([V + ".1"] if s else []), ["SD%d" % s])
+            for s in range(3):
+                scan(T.SD[:, 112 * s:112 * s + 112], T[V][:, 112 * s:112 * s + 112], T.MD[:], BIG, AL.min, AL.add,
+                     ["MD", V + ".0", V + ".1"][:3 if s else 2], ["SD%d" % s])
+
+        def rows(k):
+            dma("sy", NL[16 * k:16 * k + 16, 0:21], T.Lg[16 * k:16 * k + 16, 22 * k:22 * k + 21], "nl%d" % t, 96,
+                ["Lg%d.0" % k, "Lg%d.1" % k] if k else ["Lg0"], [] if k else ["NLd%d" % t])
 
         table(0)
         table(1)
-        grow(0, 0)
-        hold(0, 0)
-        grow(0, 1)
-        hold(0, 1)
-        hold(0, 2)
-        dma("sy", NL[0:16, :], T.Lg[0:16, 0:22], "nl%d" % t, 96, ["Lg0", "Lp0", "NL%d" % t], ["NLd%d" % t])
+        grow(0)
+        hold(0)
+        rows(0)
         for k in range(1, 8):
             V = "V%d" % (k % 2)
-            vk = [V + ".0", V + ".1"]
-            for h in range(2):
+            for h, s in ((0, 0), (0, 1), (1, 0)):
                 a, e = HV[h]
-                for s in range(2):
-                    act(T["CD%d" % h][:, s::4], T[V][:, a:e], AF.Sign, vk[0:1 + h] + ["SD%d" % s, "CD%d" % h],
-                        ["CD%d.%d" % (h, s)], bias=T.SD[:, 112 * s + 111:112 * s + 112], scale=-1.0)
+                act(T["CD%d" % h][:, s::4], T[V][:, a:e], AF.Sign, [V + ".%d" % h, "SD%d" % s],
+                    ["CD%d.%d" % (h, s)], bias=T.SD[:, 112 * s + 111:112 * s + 112], scale=-1.0)
             if k < 7:
                 table(k + 1)
             if 2 <= k < 6:
                 sort(k - 2)
+
+            def beats(h, s, two):
+                a, e = HV[h]
+                ts(T["CD%d" % h][:, s::4], T[V][:, a:e], T.SD[:, 112 * s + 111:112 * s + 112], two, AL.is_lt,
+                   AL.mult if two else None, [V + ".%d" % h, "SD%d" % s], ["CD%d.%d" % (h, s)])
+
+            beats(1, 1, 2.0)
+            beats(0, 2, None)
+            beats(1, 2, None)
+            for h in range(2):
+                n = HV[h][1] - HV[h][0]
+                quant("cd%d" % h, 0, n, T["CD%d" % h][:], ["CD%d.%d" % (h, s) for s in range(3)] + ["CD%dz" % h])
+                mm("pb%d" % h, n, "ED", 0, "cd%d" % h, 0, True, True, ["ED0", "cd%d0" % h])
             for h in range(2):
                 a, e = HV[h]
-                ts(T["CD%d" % h][:, 2::4], T[V][:, a:e], T.SD[:, 335:336], None, AL.is_lt, None,
-                   vk + ["SD2"], ["CD%d.2" % h])
-                quant("cd%d" % h, 0, e - a, T["CD%d" % h][:], ["CD%d.%d" % (h, s) for s in range(3)])
-                mm("pb%d" % h, e - a, "ED", 0, "cd%d" % h, 0, True, True, ["ED0", "cd%d0" % h])
-            for h in range(2):
-                a, e = HV[h]
-                x, y = LV[h]
-                got = T["sc%d" % h]
-                scan(got[:], T["pb%d" % h][:, 0:e - a], T.MNd[:, a:e], 4096.0, AL.min, AL.add,
+                scan(T.sc[:, a:e], T["pb%d" % h][:, 0:e - a], T.MNd[:, a:e], 4096.0, AL.min, AL.add,
                      ["pb%d" % h, "MNd"], ["sc%d" % h])
-                if k < 7 or t == R - 1:
-                    ts(lg(k, h), got[:, 15::16], bc[:, 3:4], None, AL.add, None, ["sc%d" % h, "bn"],
-                       ["Lg%d.%d" % (k, h)])
-                if k == 6:
-                    ts(T.x6[96:128, x:y], got[96:128, 15::16], bc[96:128, 9:10], bc[96:128, 11:12], AL.mult, AL.add,
-                       ["sc%d" % h, "m6", "c6"], ["x6.%d" % h])
-                if k == 7:
-                    tt(T.x7[96:128, x:y], got[96:128, 15::16], T.x6[96:128, x:y], AL.max,
-                       ["sc%d" % h, "x6.%d" % h], ["x7.%d" % h])
-                    ts(NL[96:128, x:y], T.x7[96:128, x:y], bc[96:128, 12:13], None, AL.add, None,
-                       ["x7.%d" % h, "b7", "NL%d" % t], ["NL%d.%d" % (t, h)])
-                if k < 7:
-                    grow(k, h)
-                    for s in ((0,), (1, 2))[h]:
-                        hold(k, s)
+            if k == 7:
+                tt(T.x7[96:128, 0:21], T.sc[96:128, 15::16], T.x6[96:128, 0:21], AL.max, ["sc0", "sc1", "x6"], ["x7"])
+                ts(NL[96:128, 0:21], T.x7[96:128, 0:21], bc[96:128, 12:13], None, AL.add, None, ["x7", "b7"],
+                   ["NL%d" % t])
+            if k < 7 or t == R - 1:
+                for h in range(2):
+                    a, e = HV[h]
+                    ts(T.Lg[:, 22 * k + LV[h][0]:22 * k + LV[h][1]], T.sc[:, a + 15:e:16], bc[:, 3:4], None, AL.add,
+                       None, ["sc%d" % h, "bn"], ["Lg%d.%d" % (k, h)])
+            if k == 6:
+                ts(T.x6[96:128, 0:21], T.sc[96:128, 15::16], bc[96:128, 9:10], bc[96:128, 11:12], AL.mult, AL.add,
+                   ["sc0", "sc1", "m6", "c6"], ["x6"])
+            if k < 7:
+                grow(k)
+                hold(k)
             if k < 6:
-                dma("sy", NL[16 * k:16 * k + 16, :], T.Lg[16 * k:16 * k + 16, 22 * k:22 * k + 22], "nl%d" % t, 96,
-                    ["Lg%d.0" % k, "Lg%d.1" % k, "Lp%d" % k], [])
-        zk = [["NL%d" % t, "NL%d.%d" % (t, h), "NLd%d" % t] for h in range(2)]
+                rows(k)
+        zk = ["NL%d" % t, "NLd%d" % t]
         for h in range(2):
             a, e = HV[h]
             x, y = LV[h]
             for b in range(4):
                 o, i = T.Z[:, 4 * a + b:4 * e:4], pl("G", b).indirect(NL[:, x:y])
                 if b < 2:
-                    cp(o, i, ["G%d" % b] + zk[h], ["Z%d.%d" % (h, b)])
+                    cp(o, i, ["G%d" % b] + zk, ["Z%d.%d" % (h, b)])
                 else:
-                    act(o, i, AF.Copy, ["G%d" % b] + zk[h], ["Z%d.%d" % (h, b)])
+                    act(o, i, AF.Copy, ["G%d" % b] + zk, ["Z%d.%d" % (h, b)])
             quant("z", a, e, T.Z[:, 4 * a:4 * e], ["Z%d.%d" % (h, b) for b in range(4)])
 
         def layer(h):
@@ -445,12 +453,11 @@ def rank_program(g, core, T, topo):
                 act(pl("Y", b, a, e), m, AF.Copy, ["ym%d" % b], ["Y%d.%d" % (b, h)], scale=0.03125)
 
         layer(0)
-        for h in range(2):
-            cp(T.iW[:].indirect(NL[:, LV[h][0]:LV[h][1]]), T.ji[:, HV[h][0]:HV[h][1]], ["ji"] + zk[h], ["iW"], True)
+        cp(T.iW[:].indirect(NL[:, 0:21]), T.ji[:], ["ji"] + zk, ["iW"])
         best(0)
         layer(1)
         cp(T.tm[:], T.iW[:].indirect(ll[:, 0:21]), ["iW", "ll%d" % t], ["tm"])
-        to_list(T.tm[:], "tm", bc[:, 3:4], 1.0, [(T.ML[:, 0:11], 0, 11), (T.ML[:, 12:22], 11, 21)], "ML")
+        to_list(T.tm[:], "tm", bc[:, 3:4], 1.0, T.ML[:, 0:21], "ML")
         best(1)
         for h in range(2):
             a, e = HV[h]
@@ -470,10 +477,9 @@ def rank_program(g, core, T, topo):
         for h in range(2):
             a, e = HV[h]
             for b in range(4):
-                mm("pb%d" % (4 * h + b), e - a, "EU%d" % b, 0, X, a, True, False, ["EU%d0" % b, X + "0", X + "176"])
+                mm("pb%d" % (4 * h + b), e - a, "EU%d" % b, 0, X, a, True, False, ["EU00", X + "0", X + "160"])
         if t == R - 1:
-            grow(7, 0)
-            grow(7, 1)
+            grow(7)
             tt(T.tb[0:1, :], T.V0[0:1, :], T.JR[0:1, :], AL.subtract, ["V0.0", "V0.1", "JR"], ["tb"])
             ts(T.tb[0:1, :], T.tb[0:1, :], 2.0 ** -9, 9.0 * OFF, AL.mult, AL.add, ["tb"], ["tb"])
             dma("sy", T.tot[:], T.tb[0:1, :], "out", 0, ["tb"], [])
@@ -493,8 +499,8 @@ def rank_program(g, core, T, topo):
         if t < R - 1:
             send_x(t + 1)
             for pb in ("pb0", "pb7"):
-                mm(pb, C, "uu", 0, N, 0, True, True, [N + "0", N + "176"])
-    nk = ["x20", "x2176"]
+                mm(pb, C, "uu", 0, N, 0, True, True, [N + "0", N + "160"])
+    nk = ["x20", "x2160"]
     mm("pb0", C, "v", 0, "x2", 0, True, True, ["v0"] + nk)
     dma("sy", T.oc[:], T.x2q[:].bitcast(dt.uint8), "out", 0, nk, [])
     act(T.ysb[:], T.pb0[:, 0:C], AF.Copy, ["pb0"], ["ysb"])

from concourse.mybir import dt, AluOpType, ActivationFunctionType

AL, AF = AluOpType, ActivationFunctionType
C, R = 336, 2
HV = [(0, 160), (160, 336)]
LV = [(0, 10), (10, 21)]
INF = float(2 ** 90)
TINY = float(2.0 ** -120)
BIG = float(2 ** 21)
MAGIC = 1.5 * 2.0 ** 28
OFF = 47

SCRATCH = {}


def _s(name, n, d="float32", where="sbuf"):
    SCRATCH[name] = (where, [128, n], d)


def _q(name, n):
    _s(name + "q", n, "float8_e4m3fn_x4")
    _s(name + "s", n, "uint8")


CONST = ["EU0", "EU1", "EU2", "EU3", "EG", "EA", "ED"] + ["EP%d" % _k for _k in range(8)]
for _n in ("xin", "xt0", "xt1", "Z", "Yp", "Ca", "Cb", "C5", "PT", "F", "G", "Y"):
    _s(_n, 4 * C, "bfloat16")
for _n in ("uin", "vin", "ones", "W2", "W3", "W4"):
    _s(_n, 512, "bfloat16")
_s("Eb", 512 * len(CONST), "bfloat16")
_q("E", 128 * len(CONST))
for _n in ("yt", "ym"):
    _s(_n, 4 * 176)
_s("P", 8 * C)
_s("Lg", 8 * 22, "uint16")
for _k in range(8):
    _s("pb%d" % _k, 512, "float32", "psum")
for _n, _k in (("u", 128), ("v", 128), ("uu", 256), ("wl", 1024), ("ca", C), ("cb", C), ("z", C), ("pp", C)):
    _q(_n, _k)
for _h in range(2):
    _s("CD%d" % _h, 4 * (HV[_h][1] - HV[_h][0]), "bfloat16")
    _q("cd%d" % _h, HV[_h][1] - HV[_h][0])
    _s("V%d" % _h, C)
    _s("df%d" % _h, C)
for _t in range(R):
    _q("rx%d" % _t, C)
    _q("ry%d" % _t, C)
    _q("y%d" % _t, C)
    _s("ls%d" % _t, 44, "uint16")
    _s("ll%d" % _t, 44, "uint16")
    _s("NL%d" % _t, 22, "uint16")
for _t in range(R + 1):
    _q("x%d" % _t, C)
for _n in ("jp", "ji", "d", "dn", "de", "k1", "k2", "k3", "JR", "MN", "MNd", "MH", "RH", "t1", "Hd", "sa", "oW", "iW",
           "tm", "tb", "va", "SD", "ysb", "sc"):
    _s(_n, C)
_s("hi", C, "bfloat16")
_s("lo", C, "bfloat16")
_s("MD", 112)
_s("x6", 22)
_s("x7", 22)
_s("pI", 4, "int32")
_s("oI", 16, "int32")
_s("oU", 16, "uint16")
_s("ML", 22, "uint16")
_s("bc", 32)

SEMAPHORES = ["ve", "ac", "pe", "gp", "lx", "lu", "lv", "lw", "lz", "out", "loc"]
SEMAPHORES += ["%s%d" % (a, t) for a in ("xa", "la", "nl", "ya", "yb") for t in range(R)]


def rank_program(g, core, T, topo):
    r = T.rank_of(core)
    if r is None:
        return
    queue = {"ve": g.vector, "ac": g.scalar, "pe": g.tensor, "gp": g, "sy": g.sync}
    tick = {"ve": 0, "ac": 0, "pe": 0, "gp": 0}
    known = {e: {} for e in queue}
    wr, rd, dcount, arr, sent = {}, {}, {}, {}, [0]

    def deps(e, reads, writes):
        want = {}
        for k in reads:
            for s, v in wr.get(k, {}).items():
                want[s] = max(v, want.get(s, 0))
        for k in list(writes) + [k for k in reads if k[:2] == "pb"]:
            for tab in (wr, rd):
                for s, v in tab.get(k, {}).items():
                    if s != e or tab is rd and e != "pe" and k in writes:
                        want[s] = max(v, want.get(s, 0))
        for s, v in want.items():
            if known[e].get(s, 0) < v:
                queue[e].wait_ge(T.sem[s], v)
                known[e][s] = v

    def op(e, fn, reads, writes):
        deps(e, reads, writes)
        fn(queue[e]).then_inc(T.sem[e], 1)
        tick[e] += 1
        for k in reads:
            rd.setdefault(k, {})[e] = tick[e]
        for k in writes:
            wr.setdefault(k, {})[e] = tick[e]

    def dma(e, out, in_, sem, total, reads=(), writes=()):
        deps(e, reads, writes)
        queue[e].dma_start(out, in_).then_inc(T.sem[sem], 16)
        dcount[sem] = dcount.get(sem, 0) + 16
        for k in writes:
            wr.setdefault(k, {})[sem] = total
        for k in reads:
            rd.setdefault(k, {})[sem] = total

    def tt(out, a, b, o, reads, writes):
        op("ve", lambda q: q.tensor_tensor(out, a, b, o), reads, writes)

    def ts(out, a, s1, s2, o0, o1, reads, writes):
        if o1 is None:
            op("ve", lambda q: q.tensor_scalar(out, a, s1, None, o0), reads, writes)
        else:
            op("ve", lambda q: q.tensor_scalar(out, a, s1, s2, o0, o1), reads, writes)

    def cp(out, a, reads, writes):
        op("ve", lambda q: q.tensor_copy(out, a), reads, writes)

    def fill(ap, c, key):
        op("ve", lambda q: q.memset(ap, c), [], [key])

    def scan(out, a, b, ini, o0, o1, reads, writes):
        op("ve", lambda q: q.tensor_tensor_scan(out, a, b, ini, o0, o1), reads, writes)

    def act(out, a, f, reads, writes, **k):
        op("ac", lambda q: q.activation(out, a, f, **k), reads, writes)

    def at(n):
        return ("E", 128 * CONST.index(n)) if n in CONST else (n, 0)

    def eb(n, m=1):
        k = 512 * CONST.index(n)
        return T.Eb[:, k:k + 512 * m]

    def pl(n, b, a=0, e=C):
        return T[n][:, C * b + a:C * b + e]

    def quant(name, a, b, src, reads):
        n, o = at(name)
        op("ve", lambda q: q.quantize_mx(T[n + "q"][:, o + a:o + b], T[n + "s"][:, o + a:o + b], src),
           reads, [name + str(a)])

    def mm(bank, n, st, sa, mv, ma, start, stop, reads):
        w, o = at(st)
        o += sa
        op("pe", lambda q: q.matmul_mx(T[bank][:, 0:n], T[w + "q"][:, o:o + 128], T[w + "s"][:, o:o + 128],
                                       T[mv + "q"][:, ma:ma + n], T[mv + "s"][:, ma:ma + n], start, stop),
           reads, [bank])

    def send(pc, out, in_, rsem, reads):
        deps("gp", reads, ())
        rid, pid, _e = topo.addr(pc)
        g.remote_dma(out, in_, T.sem[rsem], T.sem.loc, pid, rid, topo.mask(core, pc))
        sent[0] += len(topo.engines(core, pc))

    def arrives(keys, sem, val):
        for k in keys:
            wr.setdefault(k, {})[sem] = val
        arr[sem] = val

    def part(t):
        return T.cores[r ^ (1 << t)]

    def ne(t):
        return len(topo.engines(part(t), core))

    def send_x(t):
        send(part(t), T["rx%dq" % t][:].bitcast(dt.uint8), T["x%dq" % t][:].bitcast(dt.uint8), "xa%d" % t,
             ["x%d0" % t, "x%d160" % t])
        send(part(t), T["rx%ds" % t][:], T["x%ds" % t][:], "xa%d" % t, ["x%d0" % t])
        arrives(["rx%d" % t], "xa%d" % t, 2 * ne(t))

    dma("sy", T.xin[:], T.x[:], "lx", 16, (), ["xin"])
    dma("ac", T.uin[:], T.u[:], "lu", 16, (), ["uin"])
    dma("sy", T.wlq[:].bitcast(dt.uint8), T.wc[:], "lw", 16, (), ["w0"])
    dma("sy", T.vin[:], T.v[:], "lv", 16, (), ["vin"])
    dma("sy", T.wls[:], T.ws[:], "lz", 16, (), ["wsc"])
    f32 = dict(allow_small_or_imprecise_dtypes=True)
    bc = T.bc

    def iota(ap, pat, base, cm, key, **k):
        op("gp", lambda q: q.iota(ap, pat, base, cm, **k), [], [key])

    def sel(ap, src, pat, o, fl, base, cm, reads, key):
        op("gp", lambda q: q.affine_select(ap, src, pat, o, fl, base, cm), reads, [key])

    iota(T.pI[:, 0:1], [[1, 1]], 0, 1, "pI")
    iota(T.oI[:], [[1, 2], [16, 8]], 0, 0, "oI")
    iota(T.jp[:], [[0, 21], [1, 16]], 0, 0, "jp", **f32)
    fill(T.ones[:], 1.0, "ones")
    fill(T.k3[:], INF, "k3")
    fill(T.W4[:], 1.0, "W4")
    ts(T.W4[:, 3::4], T.W4[:, 3::4], 0.5, None, AL.mult, None, ["W4"], ["W4"])
    ts(T.pI[:, 1:2], T.pI[:, 0:1], 15, None, AL.bitwise_and, None, ["pI"], ["pI1"])
    ts(T.pI[:, 2:3], T.pI[:, 0:1], 4, None, AL.arith_shift_right, None, ["pI"], ["pI2"])
    cp(bc[:, 0:1], T.pI[:, 1:2], ["pI1"], ["i"])
    cp(T.oU[:], T.oI[:], ["oI"], ["oU"])
    ts(T.d[:], T.jp[:], bc[:, 0:1], None, AL.subtract, None, ["jp", "i"], ["d"])
    act(T.de[:], T.d[:], AF.Abs, ["d"], ["de"])
    act(T.de[:], T.de[:], AF.Relu, ["de"], ["de"], bias=1.0, scale=-1.0)
    act(T.MH[:], T.de[:], AF.Identity, ["de"], ["MH"], bias=-INF, scale=2 * INF)
    sel(T.RH[:], T.k3[:], [[0, 21], [1, 16]], AL.is_gt, -INF, 0, 0, ["k3"], "RH")
    act(T.dn[:], T.d[:], AF.Sign, ["d"], ["dn"], scale=-1.0)
    act(T.k1[:], T.dn[:], AF.Relu, ["dn"], ["k1"], scale=4096.0)
    act(T.k2[:], T.de[:], AF.Copy, ["de"], ["k2"], scale=-1024.0)
    cp(bc[:, 1:2], T.pI[:, 2:3], ["pI2"], ["g"])
    ts(bc[:, 3:4], bc[:, 0:1], 0.0, -3072.0, AL.is_equal, AL.mult, ["i"], ["bn"])
    for k, sg, b in ((4, 1.0, float(OFF)), (5, -1.0, 335.0 - OFF), (6, -1.0, 1024.0)):
        act(bc[:, k:k + 1], bc[:, 3:4], AF.Identity, ["bn"], ["b%d" % k], bias=b, scale=sg)
    fill(bc[:, 24:25], -TINY, "tiny")
    fill(bc[:, 25:26], TINY, "tiny")
    quant("u", 0, 128, T.uin[:], ["uin"])
    cp(T.uuq[:].bitcast(dt.uint32), T.uq[:].bitcast(dt.uint32).indirect(T.oU[:]), ["u0", "oU"], ["uuc"])
    act(T.uus[:], T.us[:].indirect(T.oU[:]), AF.Copy, ["u0", "oU"], ["uup"])
    quant("x0", 0, C, T.xin[:], ["xin"])
    for pb in ("pb0", "pb7"):
        mm(pb, C, "uu", 0, "x0", 0, True, True, ["uuc", "uup", "x00"])
    sel(eb("EG"), T.W4[:], [[-16, 8], [0, 64]], AL.is_ge, 0.0, 0, 1, ["W4"], "EGb")
    sel(eb("EG"), eb("EG"), [[16, 8], [0, 64]], AL.is_ge, 0.0, 15, -1, ["EGb"], "EGb")
    sel(eb("EA"), T.W4[:], [[0, 512]], AL.is_ge, 0.0, 15, -1, ["W4"], "EAb")
    send_x(0)
    iota(T.ji[:], [[1, C]], 0, 0, "ji", **f32)
    iota(T.JR[:], [[-1, C]], 512 * OFF + 511, 0, "JR", **f32)
    for b in range(4):
        sel(eb("EU%d" % b), T.ones[:], [[1, 512]], AL.is_equal, 0.0, -b, -4, ["ones"], "EU%db" % b)
    fill(T.MD[:], BIG, "MD0")
    sel(T.MD[:], T.MD[:], [[-1, 112]], AL.is_gt, 0.0, 0, 1, ["MD0"], "MD1")
    sel(T.MD[:], T.MD[:], [[1, 112]], AL.not_equal, -BIG, 0, -1, ["MD1"], "MD")

    def consts1(q):
        if q == 0:
            quant("EG", 0, 256, eb("EG", 2), ["EGb", "EAb"])
        zeros = [("C5", 1, C), ("C5", 2, C)] if q == 1 else []
        if q == 4:
            zeros = [("CD0", 3, 160), ("CD1", 3, 176), ("PT", 2, C), ("PT", 3, C)]
        for n, k, m in zeros:
            act(T[n][:, k::4], T.ones[:, 0:m], AF.Copy, ["ones"], [n + "z"], scale=0.0)
        if q in (2, 3):
            n, w = (("W3", (0.5, 0.5, 1.0, 0.0)), ("W2", (512.0, 512.0, 0.0, 0.0)))[q - 2]
            for k in range(4):
                act(T[n][:, k::4], T.ones[:, 0:128], AF.Copy, ["ones"], [n], scale=w[k])

    def consts2():
        tt(T.MN[:], T.k1[:], T.k2[:], AL.add, ["k1", "k2"], ["MN"])
        ts(T.MN[:, 15::16], T.MN[:, 15::16], bc[:, 6:7], None, AL.add, None, ["MN", "b6"], ["MN"])
        for t in range(R):
            fill(T["ls%d" % t][:], 0, "ls%d" % t)

    def consts3():
        quant("EU0", 0, 512, eb("EU0", 4), ["EU%db" % b for b in range(4)])
        act(T.k3[:, 0:160], T.de[:, 0:160], AF.Copy, ["de", "RH"], ["k3"], scale=-1024.0 + 111.5)
        act(T.k3[:, 160:C], T.de[:, 160:C], AF.Copy, ["de", "RH"], ["k3"], scale=-1024.0 + 56.0)
        tt(T.MNd[:], T.k1[:], T.k3[:], AL.add, ["k1", "k3"], ["MNd"])
        ts(T.MNd[:, 15::16], T.MNd[:, 15::16], bc[:, 6:7], None, AL.add, None, ["MNd", "b6"], ["MNd"])
        ts(T.MD[:, 111:112], T.MD[:, 111:112], BIG, None, AL.add, None, ["MD"], ["MD"])
        act(bc[:, 8:9], bc[:, 1:2], AF.Identity, ["g"], ["g6"], bias=-6.0)
        act(bc[:, 8:9], bc[:, 8:9], AF.Abs, ["g6"], ["g6"])
        act(bc[:, 9:10], bc[:, 8:9], AF.Relu, ["g6"], ["m6"], bias=1.0, scale=-1.0)
        act(bc[:, 10:11], bc[:, 9:10], AF.Copy, ["m6", "bn"], ["mb"], scale=bc[:, 3:4])
        act(bc[:, 11:12], bc[:, 9:10], AF.Identity, ["m6", "mb"], ["c6"], bias=bc[:, 10:11], scale=14096.0)
        act(bc[:, 11:12], bc[:, 11:12], AF.Identity, ["c6"], ["c6"], bias=-10000.0)
        act(bc[:, 12:13], bc[:, 9:10], AF.Identity, ["m6", "bn"], ["b7"], bias=bc[:, 3:4], scale=-4096.0)
        act(bc[:, 13:14], bc[:, 10:11], AF.Copy, ["mb"], ["nb"], scale=-1.0)
        act(bc[:, 12:13], bc[:, 12:13], AF.Identity, ["b7", "nb"], ["b7"], bias=bc[:, 13:14])
        quant("ED", 0, 128, eb("ED"), ["EDb"])

    def places(bank, counts, hook):
        S = T[bank]
        tt(T.t1[:], S[:, 0:C], T.MH[:], AL.min, [bank, "MH"], ["t1"])
        scan(T.Hd[:], T.RH[:], T.t1[:], -INF, AL.min, AL.max, ["RH", "t1"], ["Hd"])

        def count(q):
            n, k = ("C5" if q == 5 else ("Ca", "Cb")[q % 2]), ("ca", "cb")[q % 2]
            hook(q)
            quant(k, 0, C, T[n][:], [n + ".0", n + ".1", n + ".2", n + ".3"] + (["C5z"] if q == 5 else []))
            for st, pb in counts:
                mm(pb, C, st, 0, k, 0, q == 0, q == 5, [k + "0", "EG0"])

        for q in range(6):
            n = "C5" if q == 5 else ("Ca", "Cb")[q % 2]
            for k in ((3, 0, 1, 2) if q < 5 else (3,)):
                c = 4 * q + k if q < 5 else 20
                m = 16 * (c + 1)
                D = T.Hd[:, m - 1:m]
                parts = [(0, m, AL.is_lt, 24), (m, C, AL.is_le, 25)][:1 if c == 20 else 2]
                if k == 3:
                    df = "df%d" % (q % 2)
                    act(T[df][:], T.pb7[:, 0:C], AF.Identity, ["pb7", "Hd"], [df], bias=D, scale=-1.0)
                    for a, e, o, z in parts:
                        act(T[n][:, 4 * a + 3:4 * e:4], T[df][:, a:e], AF.Sign, [df, "tiny"], [n + ".3"],
                            bias=bc[:, z:z + 1])
                else:
                    for a, e, o, z in parts:
                        ts(T[n][:, 4 * a + k:4 * e:4], S[:, a:e], D, None, o, None, [bank, "Hd"], [n + ".%d" % k])
                    if k == 0 and q:
                        count(q - 1)
            if q == 5:
                tt(T[n][:, 0::4], S[:, 0:C], T.Hd[:], AL.is_equal, [bank, "Hd"], [n + ".0"])
                count(4)
                count(5)

    def to_list(src, key, bias, sign, o, okey):
        scan(T.sa[:], src, T.MN[:], 4096.0, AL.min, AL.add, [key, "MN"], ["sa"])
        ts(o, T.sa[:, 15::16], sign, bias, AL.mult, AL.add, ["sa", "bn", "b4", "b5"], [okey])

    for t in range(R):
        pc, ls, ll, NL = part(t), T["ls%d" % t], T["ll%d" % t], T["NL%d" % t]
        lk, X = "ls%d" % t, "x%d" % t
        places("pb0", [("EG", "pb2"), ("EA", "pb3")], lambda q: consts1(q) if t == 0 else None)
        if t == 0:
            consts2()
        for pb in ("pb1", "pb7"):
            mm(pb, C, "uu", 128, "rx%d" % t, 0, True, True, ["uuc", "uup", "rx%d" % t])
        to_list(T.pb2[:, 0:C], "pb2", bc[:, 4:5], 1.0, ls[:, 0:21], lk)
        cp(T.oW[:].indirect(ls[:, 0:21]), T.ji[:], [lk, "ji"], ["oW"])
        to_list(T.oW[:], "oW", bc[:, 3:4], 1.0, ls[:, 22:43], lk)
        send(pc, ll[:], ls[:], "la%d" % t, [lk])
        arrives(["ll%d" % t], "la%d" % t, ne(t))
        if t == 0:
            sel(eb("ED"), T.W3[:], [[0, 512]], AL.is_ge, 0.0, 111, -1, ["W3"], "EDb")
            for k in range(8):
                sel(eb("EP%d" % k), T.W2[:], [[0, 512]], AL.is_equal, 0.0, -16 * k, 1, ["W2"], "EP%db" % k)
        act(T.va[:], T.pb3[:, 0:C], AF.Copy, ["pb3"], ["va"], scale=512.0)
        to_list(T.pb3[:, 0:C], "pb3", bc[:, 5:6], -1.0, T.Lg[:, 0:21], "Lg0")
        tt(T.V0[:], T.va[:], T.JR[:], AL.add, ["va", "JR"], ["V0.0", "V0.1"])
        if t == 0:
            consts3()

        def unpack(q):
            if q < 4:
                pb = ("pb4", "pb5", "pb6", "pb0")[q]
                mm(pb, C, "EU%d" % q, 0, "rx%d" % t, 0, True, True, ["EU00", "rx%d" % t])
                act(pl("F", q), T[pb][:, 0:C], AF.Copy, [pb], ["F%d" % q])

        places("pb1", [("EG", "pb2")], unpack)
        if t == 0:
            for k in (0, 4):
                quant("EP%d" % k, 0, 512, eb("EP%d" % k, 4), ["EP%db" % (k + i) for i in range(4)])
        ts(T.hi[:], T.pb2[:, 0:C], MAGIC, -MAGIC, AL.add, AL.add, ["pb2"], ["hi"])
        tt(T.lo[:], T.pb2[:, 0:C], T.hi[:], AL.subtract, ["pb2", "hi"], ["lo"])
        act(T.PT[:, 0::4], T.hi[:].indirect(ll[:, 22:43]), AF.Copy, ["hi", "ll%d" % t], ["PT0"])
        cp(T.PT[:, 1::4], T.lo[:].indirect(ll[:, 22:43]), ["lo", "ll%d" % t], ["PT1"])
        quant("pp", 0, C, T.PT[:], ["PTz", "PT0", "PT1"])

        def table(k):
            pb = "pb%d" % (4 + k % 4)
            mm(pb, C, "EP%d" % k, 0, "pp", 0, True, True, ["EP%d0" % (k // 4 * 4), "pp0"])
            act(pl("P", k), T[pb][:, 0:C], AF.Copy, [pb], ["P%d" % k])

        def sort(b):
            act(pl("G", b), pl("F", b).indirect(ll[:, 22:43]), AF.Copy, ["F%d" % b, "ll%d" % t], ["G%d" % b])

        def grow(k):
            old, new = "V%d" % (k % 2), "V%d" % ((k + 1) % 2)
            for h in range(2):
                a, e = HV[h]
                tt(T[new][:, a:e], pl("P", k).indirect(T.Lg[:, 22 * k + LV[h][0]:22 * k + LV[h][1]]), T[old][:, a:e],
                   AL.add, ["P%d" % k, "Lg%d.%d" % (k, h) if k else "Lg0", old + ".%d" % h], [new + ".%d" % h])

        def hold(k):
            V = "V%d" % ((k + 1) % 2)
            for s in range(3):
                scan(T.SD[:, 112 * s:112 * s + 112], T[V][:, 112 * s:112 * s + 112], T.MD[:], BIG, AL.min, AL.add,
                     ["MD", V + ".0", V + ".1"][:3 if s else 2], ["SD%d" % s])

        def rows(k):
            dma("sy", NL[16 * k:16 * k + 16, 0:21], T.Lg[16 * k:16 * k + 16, 22 * k:22 * k + 21], "nl%d" % t, 96,
                ["Lg%d.0" % k, "Lg%d.1" % k] if k else ["Lg0"], [] if k else ["NLd%d" % t])

        table(0)
        table(1)
        grow(0)
        hold(0)
        rows(0)
        for k in range(1, 8):
            V = "V%d" % (k % 2)
            for h, s in ((0, 0), (0, 1), (1, 0)):
                a, e = HV[h]
                act(T["CD%d" % h][:, s::4], T[V][:, a:e], AF.Sign, [V + ".%d" % h, "SD%d" % s],
                    ["CD%d.%d" % (h, s)], bias=T.SD[:, 112 * s + 111:112 * s + 112], scale=-1.0)
            if k < 7:
                table(k + 1)
            if 2 <= k < 6:
                sort(k - 2)

            def beats(h, s, two):
                a, e = HV[h]
                ts(T["CD%d" % h][:, s::4], T[V][:, a:e], T.SD[:, 112 * s + 111:112 * s + 112], two, AL.is_lt,
                   AL.mult if two else None, [V + ".%d" % h, "SD%d" % s], ["CD%d.%d" % (h, s)])

            beats(1, 1, 2.0)
            beats(0, 2, None)
            beats(1, 2, None)
            for h in range(2):
                n = HV[h][1] - HV[h][0]
                quant("cd%d" % h, 0, n, T["CD%d" % h][:], ["CD%d.%d" % (h, s) for s in range(3)] + ["CD%dz" % h])
                mm("pb%d" % h, n, "ED", 0, "cd%d" % h, 0, True, True, ["ED0", "cd%d0" % h])
            for h in range(2):
                a, e = HV[h]
                scan(T.sc[:, a:e], T["pb%d" % h][:, 0:e - a], T.MNd[:, a:e], 4096.0, AL.min, AL.add,
                     ["pb%d" % h, "MNd"], ["sc%d" % h])
            if k == 7:
                tt(T.x7[96:128, 0:21], T.sc[96:128, 15::16], T.x6[96:128, 0:21], AL.max, ["sc0", "sc1", "x6"], ["x7"])
                ts(NL[96:128, 0:21], T.x7[96:128, 0:21], bc[96:128, 12:13], None, AL.add, None, ["x7", "b7"],
                   ["NL%d" % t])
            if k < 7 or t == R - 1:
                for h in range(2):
                    a, e = HV[h]
                    ts(T.Lg[:, 22 * k + LV[h][0]:22 * k + LV[h][1]], T.sc[:, a + 15:e:16], bc[:, 3:4], None, AL.add,
                       None, ["sc%d" % h, "bn"], ["Lg%d.%d" % (k, h)])
            if k == 6:
                ts(T.x6[96:128, 0:21], T.sc[96:128, 15::16], bc[96:128, 9:10], bc[96:128, 11:12], AL.mult, AL.add,
                   ["sc0", "sc1", "m6", "c6"], ["x6"])
            if k < 7:
                grow(k)
                hold(k)
            if k < 6:
                rows(k)
        zk = ["NL%d" % t, "NLd%d" % t]
        for h in range(2):
            a, e = HV[h]
            x, y = LV[h]
            for b in range(4):
                o, i = T.Z[:, 4 * a + b:4 * e:4], pl("G", b).indirect(NL[:, x:y])
                if b < 2:
                    cp(o, i, ["G%d" % b] + zk, ["Z%d.%d" % (h, b)])
                else:
                    act(o, i, AF.Copy, ["G%d" % b] + zk, ["Z%d.%d" % (h, b)])
            quant("z", a, e, T.Z[:, 4 * a:4 * e], ["Z%d.%d" % (h, b) for b in range(4)])

        def layer(h):
            a, e = HV[h]
            for b in range(4):
                for j in (1, 0):
                    mm("pb%d" % (2 * b + j), e - a, "wl", 128 * (b + 4 * j), "z", a, True, True,
                       ["w0", "wsc", "z%d" % a])
                act(T.yt[:, 176 * b:176 * b + e - a], T["pb%d" % (2 * b + 1)][:, 0:e - a], AF.Copy,
                    ["pb%d" % (2 * b + 1)], ["yt%d" % b])

        def best(h):
            a, e = HV[h]
            for b in range(4):
                m = T.ym[:, 176 * b:176 * b + e - a]
                tt(m, T["pb%d" % (2 * b)][:, 0:e - a], T.yt[:, 176 * b:176 * b + e - a], AL.max,
                   ["pb%d" % (2 * b), "yt%d" % b], ["ym%d" % b])
                act(pl("Y", b, a, e), m, AF.Copy, ["ym%d" % b], ["Y%d.%d" % (b, h)], scale=0.03125)

        layer(0)
        cp(T.iW[:].indirect(NL[:, 0:21]), T.ji[:], ["ji"] + zk, ["iW"])
        best(0)
        layer(1)
        cp(T.tm[:], T.iW[:].indirect(ll[:, 0:21]), ["iW", "ll%d" % t], ["tm"])
        to_list(T.tm[:], "tm", bc[:, 3:4], 1.0, T.ML[:, 0:21], "ML")
        best(1)
        for h in range(2):
            a, e = HV[h]
            x, y = LV[h]
            for b in range(4):
                o, i = T.Yp[:, 4 * a + b:4 * e:4], pl("Y", b).indirect(T.ML[:, x:y])
                rk = ["ML", "Y%d.0" % b, "Y%d.1" % b]
                if b < 3 - h:
                    cp(o, i, rk, ["Yp%d.%d" % (h, b)])
                else:
                    act(o, i, AF.Copy, rk, ["Yp%d.%d" % (h, b)])
            quant("y%d" % t, a, e, T.Yp[:, 4 * a:4 * e], ["Yp%d.%d" % (h, b) for b in range(4)])
            k, sm = ["y%d%d" % (t, a)], ("ya%d", "yb%d")[h] % t
            send(pc, T["ry%dq" % t][:, a:e].bitcast(dt.uint8), T["y%dq" % t][:, a:e].bitcast(dt.uint8), sm, k)
            send(pc, T["ry%ds" % t][:, a:e], T["y%ds" % t][:, a:e], sm, k)
            arrives(["ry%d.%d" % (t, h)], sm, 2 * ne(t))
        for h in range(2):
            a, e = HV[h]
            for b in range(4):
                mm("pb%d" % (4 * h + b), e - a, "EU%d" % b, 0, X, a, True, False, ["EU00", X + "0", X + "160"])
        if t == R - 1:
            grow(7)
            tt(T.tb[0:1, :], T.V0[0:1, :], T.JR[0:1, :], AL.subtract, ["V0.0", "V0.1", "JR"], ["tb"])
            ts(T.tb[0:1, :], T.tb[0:1, :], 2.0 ** -9, 9.0 * OFF, AL.mult, AL.add, ["tb"], ["tb"])
            dma("sy", T.tot[:], T.tb[0:1, :], "out", 0, ["tb"], [])
            quant("v", 0, 128, T.vin[:], ["vin"])
        N, xt = "x%d" % (t + 1), T["xt%d" % t]
        for h in range(2):
            a, e = HV[h]
            for b in range(4):
                pb = "pb%d" % (4 * h + b)
                mm(pb, e - a, "EU%d" % b, 0, "ry%d" % t, a, False, True, ["ry%d.%d" % (t, h)])
                o = xt[:, 4 * a + b:4 * e:4]
                if b > 0:
                    cp(o, T[pb][:, 0:e - a], [pb], ["xt%d.%d" % (h, b)])
                else:
                    act(o, T[pb][:, 0:e - a], AF.Copy, [pb], ["xt%d.%d" % (h, b)])
            quant(N, a, e, xt[:, 4 * a:4 * e], ["xt%d.%d" % (h, b) for b in range(4)])
        if t < R - 1:
            send_x(t + 1)
            for pb in ("pb0", "pb7"):
                mm(pb, C, "uu", 0, N, 0, True, True, [N + "0", N + "160"])
    nk = ["x20", "x2160"]
    mm("pb0", C, "v", 0, "x2", 0, True, True, ["v0"] + nk)
    dma("sy", T.oc[:], T.x2q[:].bitcast(dt.uint8), "out", 0, nk, [])
    act(T.ysb[:], T.pb0[:, 0:C], AF.Copy, ["pb0"], ["ysb"])
    for k in range(4):
        dma("sy", T.osc[4 * k:4 * k + 4, :], T.x2s[32 * k:32 * k + 4, :], "out", 0, nk, [])
    dma("ac", T.y[:], T.ysb[:], "out", 0, ["ysb"], [])
    for s in tick:
        g.wait_ge(T.sem[s], tick[s])
    for s in dcount:
        g.wait_ge(T.sem[s], dcount[s])
    for s in arr:
        g.wait_ge(T.sem[s], arr[s])
    g.wait_ge(T.sem.loc, sent[0])
